import numpy as np, ml_dtypes
CORES = [25,29,65,69,153,157,193,197]
N = 8
BF = ml_dtypes.bfloat16
V, M, L, P, TV, HS = 2048, 1024, 256, 8, 6, (1, 3, 8)
def pushed(ls, s, n):
    return np.take_along_axis(ls.reshape(N, 8, 16 * M), (s & 15) * M + (((s * s >> 5) + s + 77 * n) & (M - 1)), 2)
def parts(rng):
    kd = rng.permutation(np.arange(V) & 3); pool = np.argsort(kd, kind="stable").reshape(4, V >> 2)
    own = np.where(rng.random((N, 8, V)) < 0.02, rng.integers(0, 4, (N, 8, V)), kd); proto = rng.integers(0, 16, (N, 8, 16, 4))
    x = np.clip(np.take_along_axis(proto, own[:, :, None], 3) + rng.integers(-1, 2, (N, 8, 16, V)), 0, 15)
    ls = rng.integers(0, V, (N, 8, 16, M)); s = rng.integers(0, 4096, (N, 8, L))
    n = np.where(rng.random((N, 8, L)) < 0.5, rng.integers(15, 17, (N, 8, L)), rng.integers(0, 17, (N, 8, L)))
    return kd, pool, x, ls, s, n, rng.integers(10, 30, (N, 8)), rng.integers(0, 256, (N, 8, 16))
def spell(rng, ls, s, n, kd, pool, p):
    a = kd[pushed(ls, s, n)]; b = (a + rng.integers(1, 4, a.shape)) & 3; j = np.arange(1, 17)[:, None]; sh = (N, 8, 16, L)
    k = np.where(j % np.maximum(p, 1)[:, :, None] == 0, a[:, :, None], b[:, :, None])
    cut = np.maximum(2 * p, rng.integers(0, 17, p.shape))[:, :, None]
    k = np.where((p[:, :, None] == 0) | (j >= cut), rng.integers(0, 4, sh), k)
    return pool[k, rng.integers(0, V >> 2, sh)]
def two(a, b, p):
    j = np.arange(1, 17)[:, None]; q = np.where(p == 0, 99, p)[:, :, None]
    return np.where(j % q == 0, a[:, :, None], b[:, :, None])
def pack(x, ls, w, s, n, th, wt):
    w = np.where(np.arange(16)[:, None] < n[:, :, None, :], w, 0)
    return {"x": np.ascontiguousarray(x.reshape(N, 128, V)).astype(np.float32).astype(BF), "ls": np.ascontiguousarray(ls.reshape(N, 128, M)).astype(np.int32),
            "wd": np.ascontiguousarray(w.reshape(N, 128, L)).astype(np.int32), "nl": n.astype(np.int32), "sd": s.astype(np.int32),
            "th": np.ascontiguousarray(th.reshape(N, 8, 1)).astype(np.int32), "wt": np.ascontiguousarray(wt.reshape(N, 128, 1)).astype(np.int32)}
def setup_inputs(rng):
    kd, pool, x, ls, s, n, th, wt = parts(rng); p = rng.choice(np.array((0, 0) + HS), (N, 8, L))
    return pack(x, ls, spell(rng, ls, s, n, kd, pool, p), s, n, th, wt)
def setup_inputs_corners(rng):
    kd, pool, x, ls, s, n, th, wt = parts(rng); sh = (N, 8, L)
    ls = np.where(rng.random(ls.shape) < 0.2, rng.choice(np.array([0, V - 1]), ls.shape), ls)
    edge = np.array(sorted({0, 1, 15, 16} | {2 * h - 2 for h in HS} | {2 * h - 1 for h in HS})); p = rng.choice(np.array(HS), sh); u = rng.random(sh)
    n = np.where(u < 0.4, 2 * p - 2, np.where(u < 0.7, 2 * p - 1, rng.choice(edge, sh)))
    n[0, 0] = 0; n[N - 1, 7] = 16; n[:, 3] = rng.choice(np.array([0, 16]), (N, L))
    s = np.where(rng.random(sh) < 0.3, rng.choice(np.array([0, 15, 16, 4095]), sh), s)
    th = rng.choice(np.array([0, 1, 20, 240]), (N, 8)); wt = rng.choice(np.array([0, 1, 255]), (N, 8, 16))
    p[N - 1, 7] = 8; th[N - 1, 7] = 0
    c = int(rng.integers(1, N - 1))
    x[c] = 8 * (np.arange(V) & 1) + rng.integers(0, 3, (8, 16, V)); th[c] = 8; th[c - 1] = 240
    ls[c - 1] |= 1; ls[c] -= ls[c] & 1
    n[c - 1] = 0; n[c] = np.maximum(n[c], 1); n[c, 7, L - 1] = 0
    a = pushed(ls, s, n); u = rng.integers(0, 4, sh); own = P * np.arange(L) + rng.integers(0, P, sh)
    b = np.where(u == 0, 0, np.where(u == 1, V - 1, np.where(u == 2, own, rng.integers(0, V, sh))))
    w = two(a, b, p); w[c, :, 0] = a[c]
    return pack(x, ls, w, s, n, th, wt)
def setup_inputs_ties(rng):
    kd, pool, x, ls, s, n, th, wt = parts(rng); sh = (N, 8, L); half = V >> 3
    th = rng.integers(16, 61, (N, 8)); val = np.stack([0 * th, th, th + 1, 2 * th + 1], -1)
    loose = np.ones(V, np.int64); loose[pool[:, :half]] = 0
    e = val[:, :, kd] + loose * rng.integers(0, 17, (N, 8, V)); x = (e[:, :, None] + np.arange(16)[:, None]) >> 4
    ls = np.where(rng.random(ls.shape) < 0.8, pool[rng.integers(0, 4, ls.shape), rng.integers(0, half, ls.shape)], ls)
    p = rng.choice(np.array(HS), sh); a = kd[pushed(ls, s, n)]; b = np.array([3, 3, 0, 0])[a]
    c = np.where(rng.random(sh) < 0.6, np.array([1, 0, 3, 2])[a], np.array([2, 3, 0, 1])[a])
    k = np.where(np.arange(1, 17)[:, None] == p[:, :, None], c[:, :, None], two(a, b, p))
    return pack(x, ls, pool[k, rng.integers(0, half, k.shape)], s, n, th, wt)
def setup_inputs_again(rng):
    kd, pool, x, ls, s, n, th, wt = parts(rng)
    few = np.concatenate([np.arange(4 * P), V - 4 * P + np.arange(4 * P)])
    x = np.clip(rng.integers(0, 16, (N, 8, 16, 1)) + rng.integers(-3, 4, (N, 8, 16, V)), 0, 15); th = rng.integers(24, 44, (N, 8))
    ls = few[rng.integers(0, 8 * P, ls.shape)]; w = few[rng.integers(0, 8 * P, (N, 8, 16, L))]
    q = int(rng.integers(0, N)); n[q] = np.maximum(n[q], 1); w[q, :, 0] = pushed(ls, s, n)[q]
    return pack(x, ls, w, s, n, th, wt)
def setup_inputs_spread(rng):
    sh = (N, 8, L)
    x = np.minimum((np.exp2(4 * rng.random((N, 8, 1, V))) * rng.random((N, 8, 16, V))).astype(np.int64), 15)
    ls = np.minimum((V * rng.random((N, 8, 16, M)) * np.sqrt(rng.random((N, 8, 16, M)))).astype(np.int64), V - 1)
    w = np.minimum((np.exp2(np.log2(V) * rng.random((N, 8, 16, L)))).astype(np.int64), V - 1)
    s = np.where(rng.random(sh) < 0.5, rng.integers(0, 4096, sh), np.minimum(np.exp2(12 * rng.random(sh)).astype(np.int64), 4095))
    wt = np.minimum(np.exp2(8 * rng.random((N, 8, 16))).astype(np.int64) - 1, 255)
    return pack(x, ls, w, s, rng.integers(0, 17, sh), rng.integers(0, 241, (N, 8)), wt)
def setup_inputs_ends(rng):
    sh = (N, 8, L)
    u = rng.integers(0, 3, (N, 8, 1, V)); x = 15 * np.where(u == 2, rng.integers(0, 2, (N, 8, 16, V)), u)
    x[:, 1:7:2, :, 0] = 0; x[:, 1:7:2, :, V - 1] = 15; x[:, 7, :, 0] = 0; x[:, 7, :, V - 1] = 15; x[:, 0, :, 0] = 15; x[:, 0, :, V - 1] = 0
    ls = (V - 1) * rng.integers(0, 2, (N, 8, 16, M)); s = 4095 * rng.integers(0, 2, sh); n = 16 * (rng.random(sh) < 0.75).astype(np.int64)
    th = 240 * rng.integers(0, 2, (N, 8)); th[:, 7] = 0; th[:, 6] = 240
    wt = 255 * rng.integers(0, 2, (N, 8, 16)); wt[:, 7] = 255; wt[:, 0] = 0
    p = rng.choice(np.array((0,) + HS), sh)
    for i, k in ((0, 0), (1, 8), (7, 0), (10, 8), (L - 2, 8), (L - 1, 0)):
        s[:, 7, i] = 4095; n[:, 7, i] = 16; p[:, 7, i] = k
    ls[:, 7, 15, ((4095 * 4095 >> 5) + 4095 + 77 * 16) & (M - 1)] = V - 1
    a = pushed(ls, s, n)
    return pack(x, ls, two(a, V - 1 - a, p), s, n, th, wt)
def check_inputs(d):
    bad = []
    for k, lo, hi in (("x", 0, 15), ("ls", 0, V - 1), ("wd", 0, V - 1), ("nl", 0, 16), ("sd", 0, 4095), ("th", 0, 240), ("wt", 0, 255)):
        v = np.asarray(d[k]).astype(np.float64)
        if not np.all((v >= lo) & (v <= hi)): bad.append("range of " + k)
        if not np.all(v == np.floor(v)): bad.append("whole numbers in " + k)
    w = np.asarray(d["wd"]).reshape(N, 8, 16, L); n = np.asarray(d["nl"]).reshape(N, 8, 1, L)
    if np.any((np.arange(16)[:, None] >= n) & (w != 0)): bad.append("empty rows of wd")
    return bad
def reference(x, ls, wd, nl, sd, th, wt):
    X = x.astype(np.float32).astype(np.int32).reshape(N, 8, 16, V); tab = ls.astype(np.int64).reshape(N, 8, 16 * M)
    w = wd.astype(np.int64).reshape(N, 8, 16, L); n = nl.astype(np.int64); s = sd.astype(np.int64)
    lim = th.astype(np.int64).reshape(N, 8, 1, 1); wgt = wt.astype(np.int64).reshape(N, 8, 16, 1)
    A = np.zeros(N, np.int64); row = np.arange(16)[:, None]
    for t in range(TV):
        new = np.take_along_axis(tab, (s & 15) * M + (((s * s >> 5) + s + 77 * n) & (M - 1)), 2)
        w = np.concatenate([new[:, :, None], w[:, :, :15]], axis=2); n = np.minimum(n + 1, 16)
        G = np.take_along_axis(X, w.reshape(N, 8, 1, 16 * L), 3).reshape(N, 8, 16, 16, L)
        bound = lim + (A & 15).reshape(N, 1, 1, 1); h = np.zeros((N, 8, L), np.int64)
        for k in HS:
            D = np.add.reduce(np.abs(G[:, :, :, :k] - G[:, :, :, k:2 * k]), axis=2)
            h = np.where((h == 0) & (2 * k <= n) & np.all(D <= bound, axis=2), k, h)
        hit = h > 0
        z = np.maximum.reduce(np.where(row < h[:, :, None, None, :], G, 0), axis=3)
        tot = np.add.reduce(wgt * np.where(hit[:, :, None], z, G[:, :, :, 0]), axis=2)
        s = np.where(hit, tot + h, 5 * s + tot) & 4095
        at = row + h[:, :, None, :]
        w = np.where(at < 16, np.take_along_axis(w, np.minimum(at, 15), 2), 0); n = n - h
        col = np.roll(P * np.arange(L) + (s & (P - 1)), 1, axis=0)[:, :, None]
        old = np.take_along_axis(X, col, 3)
        val = np.where(np.roll(hit, 1, axis=0)[:, :, None], (old + np.roll(z, 1, axis=0)) >> 1, old)
        np.put_along_axis(X, col, val.astype(np.int32), 3)
        A = np.add.reduce(hit.astype(np.int64).reshape(N, 8 * L), axis=1)
        if t < TV - 1:
            by = 1 + (t + 1) // N - t // N
            w, n, s = [np.roll(np.roll(v, 1, axis=0), by, axis=1) for v in (w, n, s)]
    return {"yx": X.reshape(N, 128, V).astype(np.float32).astype(BF), "yw": w.reshape(N, 128, L).astype(np.float32), "yn": n.astype(np.float32), "ys": s.astype(np.float32)}

@@ -1,0 +1,528 @@
+from concourse.bass import DstId, RemoteDMATransfer
+from concourse.mybir import AluOpType as A, AxisListType, ActivationFunctionType as AF
+
+TV = 6
+NX = 2304
+NH = 2064
+MATS = ("LOs", "LOq", "HIe", "HIo", "LOe", "LOo", "M1", "LOe0", "LOo0", "HIe0", "HIo0", "M10", "eye", "neg", "N0", "N1", "one")
+SCRATCH = {}
+for _t in range(TV):
+    SCRATCH["xb%d" % _t] = ("sbuf", [128, NX], "bfloat16")
+    SCRATCH["hl%d" % _t] = ("sbuf", [128, NH], "bfloat16")
+for _m in MATS:
+    SCRATCH[_m] = ("sbuf", [128, 128], "bfloat16")
+for _b in range(8):
+    SCRATCH["pb%d" % _b] = ("psum", [128, 512], "float32")
+for _n, _w, _d in (
+        ("xf", NX, "bfloat16"), ("xr", 2048, "bfloat16"), ("lsi", 1024, "int32"), ("lsH", 1024, "bfloat16"), ("lsL", 1024, "bfloat16"),
+        ("TL", 16384, "bfloat16"), ("win", 2560, "bfloat16"), ("whl", 512, "bfloat16"), ("wdi", 256, "int32"),
+        ("G", 2048, "bfloat16"), ("d8", 2048, "bfloat16"), ("P", 2048, "bfloat16"), ("RM", 2048, "bfloat16"), ("Zc", 1024, "bfloat16"),
+        ("ab13", 1024, "bfloat16"), ("SelH", 256, "bfloat16"), ("SelL", 256, "bfloat16"), ("R", 256, "bfloat16"),
+        ("ll", 128, "uint16"), ("lh", 128, "uint16"), ("zl", 16, "uint16"), ("col", 16, "uint16"), ("wl", 16, "uint16"), ("cl", 16, "uint16"),
+        ("zz", 256, "bfloat16"), ("oldh", 256, "bfloat16"), ("zf", 256, "bfloat16"), ("cf", 16, "uint16"),
+        ("roll", 128, "float32"), ("Q1", 144, "bfloat16"), ("QW", 144, "bfloat16"), ("rollb", 128, "bfloat16"),
+        ("dif", 128, "int32"), ("mi", 144, "int32"), ("pc", 1, "int32"), ("cI", 2, "int32"), ("cF", 16, "float32"),
+        ("bi", 16, "int32"), ("iB", 16, "int32"), ("i8", 16, "int32"), ("iBd", 16, "float32"),
+        ("KT", 64, "float32"), ("TAGC", 64, "float32"), ("TAG", 64, "float32"),
+        ("s4", 64, "int32"), ("sq", 64, "int32"), ("u", 64, "int32"), ("f", 64, "int32"), ("cand", 64, "float32"),
+        ("c13", 64, "float32"), ("e13", 32, "float32"), ("E", 16, "float32"), ("M8", 128, "float32"), ("c8", 16, "float32"),
+        ("SF", 16, "float32"), ("SI", 16, "int32"), ("SrI", 16, "int32"), ("k1", 16, "int32"), ("k2", 16, "int32"), ("k3", 16, "int32"),
+        ("kf", 16, "float32"), ("sI", 16, "int32"), ("nF", 16, "float32"), ("f1", 16, "bfloat16"), ("f2", 16, "bfloat16"), ("f3", 16, "bfloat16"),
+        ("npb", 16, "bfloat16"), ("Bc", 1, "float32"), ("aI", 1, "int32"), ("amo", 16, "int32"), ("ami", 16, "int32"),
+        ("CH", 128, "bfloat16"), ("e77", 128, "bfloat16"),
+        ("nsd", 512, "int32"), ("src8", 768, "bfloat16"), ("e8", 144, "bfloat16"), ("br", 128, "bfloat16"), ("m4", 128, "int32"),
+        ("thi", 1, "int32"), ("thb", 1, "bfloat16"), ("wti", 1, "int32"),
+        ("IND", 32, "float32"), ("nls", 16, "uint16"), ("hs", 256, "float32"), ("yws", 256, "float32"), ("ywr", 256, "float32"),
+        ("nst", 32, "float32"), ("nsx", 32, "float32"), ("nsr", 32, "float32"), ("xo", 2048, "bfloat16")):
+    SCRATCH[_n] = ("sbuf", [128, _w], _d)
+SCRATCH["ab8"] = ("sbuf", [128, 16, 128], "bfloat16")
+
+RING = ["x%d" % t for t in range(1, TV)] + ["h%d" % t for t in range(1, TV)] + ["a%d" % t for t in range(1, TV)]
+FIN = ["xf", "zf", "cf", "yf", "nf"]
+SEMAPHORES = (["V", "S", "P", "G", "L"] + ["r_" + n for n in RING + FIN] + ["tl%d" % t for t in range(TV)] + ["tlb"] + ["wi%d" % t for t in range(TV)]
+              + ["i_" + n for n in ("x", "ls", "wd", "ns", "th", "wt")] + ["o_" + n for n in ("x0", "x1", "w", "ns", "nt")])
+
+
+def message(name):
+    if name in FIN:
+        return {"xf": (-5, "xb5", "xf", 256, 2048, 4, 0), "zf": (-6, "zz", "zf", 0, 256, 1, 0), "cf": (-6, "col", "cf", 0, 16, 1, 1),
+                "yf": (-5, "yws", "ywr", 0, 256, 1, 2), "nf": (-5, "nsx", "nsr", 0, 32, 1, 3)}[name]
+    t = int(name[1:])
+    return {"x": (1, "xb%d" % (t - 1), "xb%d" % t, 256, 2048, 4, 0), "h": (1, "hl%d" % (t - 1), "hl%d" % t, 0, NH, 4, 0),
+            "a": (1, "amo", "ami", 2 * t, 2, 1, 1)}[name[0]]
+
+
+def order():
+    o = ["x1", "h1", "h2"]
+    for t in range(1, TV):
+        o.append("a%d" % t)
+        o.append("x%d" % (t + 1) if t + 1 < TV else "xf")
+        if t + 2 < TV:
+            o.append("h%d" % (t + 2))
+    return o + ["zf", "cf", "yf", "nf"]
+
+
+def route(name, src, dst, topo):
+    _, _, _, c0, w, pieces, first = message(name)
+    if topo.may_write(src, dst):
+        return [(None, c0, w)]
+    hs = [h for h in topo.cores_of(src) if topo.may_write(h, dst)]
+    hs = [h for h in hs if topo.die(h) == topo.die(src)] + [h for h in hs if topo.die(h) != topo.die(src)]
+    pieces = min(pieces, len(hs))
+    pick = hs[first % len(hs):] + hs[:first % len(hs)]
+    return [(pick[j], c0 + w // pieces * j, w // pieces) for j in range(pieces)]
+
+
+def peer(name, rank):
+    return (rank - message(name)[0]) % 8
+
+
+def put(g, T, topo, core, dst, sem, out, in_):
+    rid, pid = topo.addr(dst, core)
+    g.remote_dma(out, in_, T.sem[sem], T.sem.L, pid, rid, topo.mask(core, dst))
+    return len(topo.engines(core, dst))
+
+
+def helper_program(g, core, T, topo):
+    sent = 0
+    for name in order():
+        for r in range(8):
+            src, dst = T.cores[r], T.cores[peer(name, r)]
+            way = route(name, src, dst, topo)
+            for h, c0, w in way:
+                if h == core:
+                    buf = T[message(name)[2]]
+                    g.wait_ge(T.sem["r_" + name], len(topo.engines(src, core)) // len(way))
+                    sent += put(g, T, topo, core, dst, "r_" + name, buf[:, c0:c0 + w], buf[:, c0:c0 + w])
+    if sent:
+        g.wait_ge(T.sem.L, sent)
+
+
+def rank_program(g, core, T, topo):
+    rank = T.rank_of(core)
+    if rank is None:
+        return helper_program(g, core, T, topo)
+    Q = {"V": g.vector, "S": g.scalar, "P": g.tensor, "G": g, "Y": g.sync}
+    cnt, seen, last, read, bank = {q: 0 for q in Q}, {q: {} for q in Q}, {}, {}, {}
+    total = {}
+
+    def need(q, tok):
+        sem, val = tok[0], tok[1]
+        if seen[q].get(sem, 0) < val:
+            Q[q].wait_ge(T.sem[sem], val)
+            seen[q][sem] = val
+
+    def deps(q, R, W, B, dma):
+        for k in R:
+            if k in last:
+                need(q, last[k])
+        for k in W:
+            for tok in ([last[k]] if k in last else []) + list(read.get(k, {}).values()):
+                need(q, tok)
+        for b in B:
+            for q2, tok in bank.get(b, {}).items():
+                if q2 != q:
+                    need(q, tok)
+
+    def note(q, tok, R, W, B):
+        for k in W:
+            last[k] = tok
+            read[k] = {}
+        for k in R:
+            if k not in W:
+                read.setdefault(k, {})[(tok[2], tok[0])] = tok
+        for b in B:
+            bank.setdefault(b, {})[q] = tok
+
+    def run(q, call, R=(), W=(), B=()):
+        deps(q, R, W, B, False)
+        cnt[q] += 1
+        call().then_inc(T.sem[q], 1)
+        total[q] = cnt[q]
+        note(q, (q, cnt[q], q), R, W, B)
+
+    def dma(q, sem, pairs, R=(), W=()):
+        deps(q, R, W, (), True)
+        for out, in_ in pairs:
+            Q[q].dma_start(out, in_).then_inc(T.sem[sem], 16)
+            total[sem] = total.get(sem, 0) + 16
+        note(q, (sem, total[sem], None), R, W, ())
+
+    sent = [0]
+
+    def send(name, R):
+        dst = T.cores[peer(name, rank)]
+        sb, db = message(name)[1:3]
+        deps("G", R, (), (), True)
+        way = route(name, core, dst, topo)
+        if len(way) == 1:
+            h, c0, w = way[0]
+            sent[0] += put(g, T, topo, core, dst if h is None else h, "r_" + name, T[db][:, c0:c0 + w], T[sb][:, c0:c0 + w])
+            return
+        trs = []
+        for j, (h, c0, w) in enumerate(way):
+            es = topo.engines(core, h)
+            es = es[j * (len(es) // len(way)):(j + 1) * (len(es) // len(way))]
+            rid, pid = topo.addr(h, core)
+            trs.append(RemoteDMATransfer(dst_ids=[DstId(rid=rid, pnc=pid)], dma_engine_mask=sum(1 << e for e in es),
+                                         remote_sem=T.sem["r_" + name], srcs=[T[sb][:, c0:c0 + w]], dsts=[T[db][:, c0:c0 + w]]))
+            sent[0] += len(es)
+        g.remote_dma_fused(trs, local_sem=T.sem.L)
+
+    def landing(name, key):
+        src = T.cores[(rank + message(name)[0]) % 8]
+        n = 0
+        for h, _, _ in route(name, src, core, topo):
+            n += len(topo.engines(src if h is None else h, core))
+        last[key] = ("r_" + name, n, None)
+        read[key] = {}
+        total["r_" + name] = n
+
+    def ts(out, in0, s1, s2, op0, op1=None, R=(), W=(), B=()):
+        if op1 is None:
+            run("V", lambda: g.vector.tensor_scalar(out, in0, s1, None, op0), R, W, B)
+        else:
+            run("V", lambda: g.vector.tensor_scalar(out, in0, s1, s2, op0, op1), R, W, B)
+
+    def tt(out, a, b, op, R=(), W=(), B=()):
+        run("V", lambda: g.vector.tensor_tensor(out, a, b, op), R, W, B)
+
+    def cp(out, in_, R=(), W=(), B=()):
+        run("V", lambda: g.vector.tensor_copy(out, in_), R, W, B)
+
+    def fill(out, c, W, R=()):
+        run("V", lambda: g.vector.memset(out, c), R, W)
+
+    def act(out, in_, func=AF.Copy, R=(), W=(), B=(), **kw):
+        run("S", lambda: g.scalar.activation(out, in_, func, **kw), R, W, B)
+
+    def mm(out, l, r, start, stop, R=(), B=()):
+        run("P", lambda: g.tensor.matmul(out, l, r, start, stop), R, (), B)
+
+    def msum(out, bk, parts):
+        for j, (l, r, keys) in enumerate(parts):
+            mm(out, l, r, j == 0, j == len(parts) - 1, keys, (bk,))
+
+    dma("S", "i_ls", [(T.lsi[:], T.ls[:])], W=["lsi"])
+    dma("Y", "i_ns", [(T.nsd[0:8, 0:256], T.nl[:]), (T.nsd[0:8, 256:512], T.sd[:])], W=["nsd"])
+    dma("Y", "i_wd", [(T.wdi[:], T.wd[:])], W=["wdi"])
+    dma("Y", "i_x", [(T.xr[:], T.x[:])], W=["xr"])
+    dma("Y", "i_th", [(T.thi[0:8, :], T.th[:])], W=["thi"])
+    dma("Y", "i_wt", [(T.wti[:], T.wt[:])], W=["wti"])
+    run("G", lambda: g.iota(T.pc[:], [[0, 1]], 0, 1), (), ["pc"])
+    run("G", lambda: g.iota(T.dif[:], [[1, 128]], 256, -1), (), ["dif"])
+    run("G", lambda: g.iota(T.mi[:], [[1, 144]], 0, 0), (), ["mi"])
+    run("G", lambda: g.iota(T.bi[:], [[16, 16]], 0, 0), (), ["bi"])
+    fill(T.RM[:], 1.0, ["RM"])
+    fill(T.RM[:, 0:2048:8], 0.0, ["RM"])
+    fill(T.TL[:, 0:11264], 0.0, ["TLa"])
+    cp(T.lsH[:], T.lsi[:], R=["lsi"], W=["lsH"])
+    tt(T.lsL[:], T.lsi[:], T.lsH[:], A.subtract, R=["lsi", "lsH"], W=["lsL"])
+    for lo, hi in ((11264, 13312), (13312, 15360), (15360, 16384)):
+        act(T.TL[:, lo:hi], T.RM[:, 0:hi - lo], R=["RM"], W=["TLb"], scale=0.0)
+    zero = ["TLa", "TLb"]
+    dma("Y", "tl0", [(T.TL[a::16, 1024 * a:1024 * a + 1024], T.lsH[a::16, :]) for a in range(16)], R=zero + ["lsH"], W=["TL"])
+    dma("Y", "tlb", [(T.TL[(a + 8) % 16::16, 1024 * a:1024 * a + 1024], T.lsL[a::16, :]) for a in range(16)], R=zero + ["lsL"], W=["TLx"])
+    act(T.xb0[:, 256:NX], T.xr[:], R=["xr"], W=["xb0"], bias=128.0)
+
+    cF = T.cF
+
+    def col(j):
+        return cF[:, j:j + 1]
+    ts(T.cI[:, 0:1], T.pc[:], 15, None, A.bitwise_and, R=["pc"], W=["cI"])
+    ts(T.cI[:, 1:2], T.pc[:], 112, None, A.bitwise_and, R=["pc"], W=["cI1"])
+    cp(cF[:, 0:2], T.cI[:], R=["cI", "cI1"], W=["c0"])
+    ts(T.dif[:], T.dif[:], 127, None, A.bitwise_and, R=["dif"], W=["dif"])
+    ts(col(2), col(1), 15.0, None, A.add, R=["c0"], W=["c2"])
+    ts(col(3), col(0), 8.0, None, A.is_lt, R=["c0"], W=["c3"])
+    ts(col(4), col(0), 8.0, None, A.is_ge, R=["c0"], W=["c4"])
+    ts(col(6), col(0), 1.0, None, A.is_ge, R=["c0"], W=["c6"])
+    ts(col(7), col(0), 7.0, None, A.is_lt, R=["c0"], W=["c7"])
+    ts(col(9), col(0), 15.0, None, A.is_lt, R=["c0"], W=["c9"])
+    ts(col(11), T.pc[:], 16.0, 15.0, A.mult, A.add, R=["pc"], W=["c11"])
+    cp(col(12), T.pc[:], R=["pc"], W=["c12"])
+    tt(col(5), col(6), col(3), A.mult, R=["c6", "c3"], W=["c5"])
+    tt(col(8), col(9), col(7), A.subtract, R=["c9", "c7"], W=["c8"])
+    ts(T.e8[0:8, :], T.mi[0:8, :], cF[0:8, 11:12], None, A.is_equal, R=["mi", "c11"], W=["e8"])
+    ts(T.m4[0:8, :], T.mi[0:8, 0:128], 4, None, A.logical_shift_right, R=["mi"], W=["m4"])
+    ts(T.br[0:8, :], T.m4[0:8, :], cF[0:8, 12:13], None, A.is_equal, R=["m4", "c12"], W=["br"])
+    ts(T.iB[:], T.bi[:], col(0), None, A.add, R=["bi", "c0"], W=["iB"])
+    ts(T.i8[:], T.iB[:], 8.0, 256.0 - 16384.0, A.mult, A.add, R=["iB"], W=["i8"])
+    ts(T.iBd[:], T.iB[:], 1.0 / 512, None, A.mult, R=["iB"], W=["iBd"])
+
+    def mat(name, d, c):
+        ts(T[name][:], T.dif[:], float(d), col(c), A.is_equal, A.mult, R=["dif", "c%d" % c], W=[name])
+
+    def places0():
+        ts(T.k2[:], T.sI[:], 15, None, A.bitwise_and, R=["sI"], W=["k2"])
+        tt(T.k1[:], T.sI[:], T.sI[:], A.mult, R=["sI"], W=["k1"])
+        ts(T.k1[:], T.k1[:], 5, None, A.logical_shift_right, R=["k1"], W=["k1"])
+        tt(T.k1[:], T.k1[:], T.sI[:], A.add, R=["k1", "sI"], W=["k1"])
+        ts(T.k3[:], T.nF[:], 77.0, None, A.mult, R=["nF"], W=["k3"])
+        tt(T.k1[:], T.k1[:], T.k3[:], A.add, R=["k1", "k3"], W=["k1"])
+        ts(T.k1[:], T.k1[:], 1023, None, A.bitwise_and, R=["k1"], W=["k1"])
+        ts(T.k2[:], T.k2[:], 1024.0, None, A.mult, R=["k2"], W=["k2"])
+        tt(T.k1[:], T.k1[:], T.k2[:], A.add, R=["k1", "k2"], W=["k1"])
+        cp(T.cl[:], T.k1[:], R=["k1"], W=["cl"])
+        cp(T.SelH[:], T.wdi[:], R=["wdi"], W=["SelH"])
+        tt(T.SelL[:], T.wdi[:], T.SelH[:], A.subtract, R=["wdi", "SelH"], W=["SelL"])
+        ts(T.npb[:], T.nF[:], 1.0, 16.0, A.add, A.min, R=["nF"], W=["npb"])
+        fill(T.CH[:], 0.0, ["CH"])
+        for j, h in enumerate((1, 3, 8)):
+            fill(T.CH[:, 16 * j:16 * j + 16], -2.0 * h, ["CH"])
+            fill(T.CH[:, 64 + 16 * j:80 + 16 * j], -77.0 * h, ["CH"])
+        ts(T.e77[:], T.dif[:], 0.0, 77.0, A.is_equal, A.mult, R=["dif"], W=["e77"])
+        ts(T.KT[:, 48:64], T.sI[:], 5.0, None, A.mult, R=["sI"], W=["KT3"])
+        mat("HIe0", 121, 8)
+        mat("HIo0", 1, 8)
+        mat("M10", 1, 9)
+        ts(T.eye[:], T.dif[:], 0.0, None, A.is_equal, R=["dif"], W=["eye"])
+        ts(T.neg[:], T.dif[:], 0.0, -1.0, A.is_equal, A.mult, R=["dif"], W=["neg"])
+        ts(T.Q1[:], T.mi[:], col(2), None, A.is_equal, R=["mi", "c2"], W=["Q1"])
+    mat("LOs", 0, 3)
+    mat("LOq", 8, 3)
+    mat("HIe", 120, 4)
+    mat("HIo", 0, 4)
+    cp(T.src8[0:8, 0:512], T.nsd[0:8, :], R=["nsd"], W=["src8"])
+    tt(T.src8[0:8, 512:768], T.nsd[0:8, 256:512], T.src8[0:8, 256:512], A.subtract, R=["nsd", "src8"], W=["src8b"])
+    msum(T.pb7[:, 0:48], 7, [(T.e8[0:8, 15 - a:143 - a], T.src8[0:8, a:768:16], ["e8", "src8", "src8b"]) for a in range(16)])
+    mat("LOe0", 1, 7)
+    mat("LOo0", 9, 7)
+    ts(T.N0[:], T.mi[:, 0:128], col(1), None, A.is_equal, R=["mi", "c0"], W=["N0"])
+    ts(T.N1[:], T.mi[:, 0:128], 8.0, col(1), A.subtract, A.is_equal, R=["mi", "c0"], W=["N1"])
+    cp(T.nF[:], T.pb7[:, 0:16], W=["nF"], B=(7,))
+    cp(T.sI[:], T.pb7[:, 16:32], W=["sI"], B=(7,))
+    tt(T.sI[:], T.pb7[:, 32:48], T.sI[:], A.add, R=["sI"], W=["sI"], B=(7,))
+    places0()
+    for b, l1, l2 in ((0, "LOs", "LOq"), (1, "HIo", "HIe")):
+        for h in range(2):
+            o = 2 * b + h
+            sl = slice(512 * h, 512 * h + 512)
+            msum(T["pb%d" % o][:, 0:512], o, [(T[l1][:], T.lsH[:, sl], [l1, "lsH"]), (T[l2][:], T.lsL[:, sl], [l2, "lsL"])])
+    for o in range(4):
+        act(T.hl0[:, 512 * o:512 * o + 512], T["pb%d" % o][:, 0:512], W=["hl0_%d" % o], B=(o,))
+    cp(T.thb[0:8, :], T.thi[0:8, :], R=["thi"], W=["thb"])
+    mm(T.pb6[:, 0:1], T.br[0:8, :], T.thb[0:8, :], True, True, ["br", "thb"], (6,))
+    fill(T.hl0[:, 2050:NH], 0.0, ["hl0"])
+    cp(T.hl0[:, 2048:2049], T.wti[:], R=["wti"], W=["hl0w"])
+    cp(T.hl0[:, 2049:2050], T.pb6[:, 0:1], W=["hl0h"], B=(6,))
+    HL0 = ["hl0", "hl0w", "hl0h"] + ["hl0_%d" % o for o in range(4)]
+
+    def table(t):
+        hl = T["hl%d" % t]
+        dma("Y", "tl%d" % t, [(T.TL[p::8, 1024 * (p + 8 * j):1024 * (p + 8 * j) + 1024], hl[p::8, 1024 * j:1024 * j + 1024])
+                              for p in range(8) for j in range(2)],
+            R=["hl%d" % t], W=["TL", "TLx"])
+    send("x1", ["xb0", "TL"])
+    send("h1", HL0)
+    for t in range(1, TV):
+        landing("x%d" % t, "xb%d" % t)
+        landing("h%d" % t, "hl%d" % t)
+        landing("a%d" % t, "am%d" % t)
+        fill(T["xb%d" % t][:, 0:256], 128.0, ["xt%d" % t])
+    for n, k in (("xf", "xf"), ("zf", "zf"), ("cf", "cf"), ("yf", "ywr"), ("nf", "nsr")):
+        landing(n, k)
+    mat("LOe", 0, 5)
+    mat("LOo", 8, 5)
+    mat("M1", 0, 6)
+    for j, (h, v) in enumerate(((1, -2.0 ** 24), (3, -2.0 ** 24 + 2.0 ** 22), (8, -2.0 ** 24 + 2.0 ** 23), (0, 0.0))):
+        fill(T.TAGC[:, 16 * j:16 * j + 16], v, ["TAGC"])
+        if j < 3:
+            fill(T.KT[:, 16 * j:16 * j + 16], float(h), ["KT"])
+    fill(T.TAG[:], 0.0, ["TAG"])
+    fill(T.win[:, 1536:2048], 0.0, ["win3"])
+    ts(T.roll[:], T.dif[:], 16.0, None, A.is_equal, R=["dif"], W=["roll"])
+    ts(T.rollb[:], T.dif[:], 16.0, None, A.is_equal, R=["dif"], W=["rollb"])
+    fill(T.one[:], 1.0, ["one"])
+    fill(T.amo[:], 0.0, ["amo"])
+    fill(T.xf[:, 0:256], 128.0, ["xft"])
+
+    BIG = 5.0 * 2.0 ** 22
+    PAIRS = ((0, 1), (0, 3), (1, 4), (2, 5))
+
+    def places(S, key):
+        ts(T.k1[:], S[:], 22, None, A.arith_shift_right, R=[key], W=["k1"])
+        tt(T.kf[:], T.k1[:], T.iBd[:], A.add, R=["k1", "iBd"], W=["kf"])
+        ts(T.wl[:], T.kf[:], 512.0, 2048.0, A.mult, A.add, R=["kf"], W=["wl"])
+
+    def squares():
+        ts(T.f1[:], T.SF[:], 0.0, -8.0, A.is_lt, A.mult, R=["SF"], W=["f1"])
+
+    def lengths(where):
+        ts(T.f2[:], T.SF[:], -2.0 ** 23, 5.0, A.is_lt, A.mult, R=["SF"], W=["f2"])
+        ts(T.f3[:], T.SF[:], -3.0 * 2.0 ** 22, 2.0, A.is_lt, A.mult, R=["SF"], W=["f3"])
+        msum(T.pb2[:, 0:16], 2, [(T[where][:], T[k][:], [where, k]) for k in ("npb", "f1", "f2", "f3")])
+
+    for t in range(TV):
+        end = t == TV - 1
+        xb, kx = T["xb%d" % t], ["xb%d" % t]
+        x = xb[:, 256:NX]
+        hl, kh = T["hl%d" % t], HL0 if t == 0 else ["hl%d" % t]
+        LE, LO_, HE, HO, MW = ("LOe0", "LOo0", "HIe0", "HIo0", "M10") if t == 0 else ("LOe", "LOo", "HIe", "HIo", "M1")
+        act(T.R[:], T.TL[:].indirect(T.cl[:]), R=["TL", "TLx", "cl"], W=["R"])
+        if t:
+            act(T.SelH[:], T.win[:].indirect(T.wl[:]), R=["win", "win3", "wl"], W=["SelH"])
+            act(T.SelL[:], T.win[:, 256:2560].indirect(T.wl[:]), R=["win", "win3", "wl"], W=["SelL"])
+        ev, od = slice(0, 256, 2), slice(1, 256, 2)
+        msum(T.pb5[:, 0:128], 5, [(T.N0[:], T.R[:, ev], ["N0", "R"]), (T.N1[:], T.R[:, od], ["N1", "R"]),
+                                  (T[LE][:], T.SelH[:, ev], [LE, "SelH"]), (T[LO_][:], T.SelH[:, od], [LO_, "SelH"]),
+                                  (T[LE][:], T.SelL[:, ev], [LE, "SelL"]), (T[LO_][:], T.SelL[:, od], [LO_, "SelL"])])
+        msum(T.pb6[:, 0:128], 6, [(T[HE][:], T.SelH[:, ev], [HE, "SelH"]), (T[HO][:], T.SelH[:, od], [HO, "SelH"]),
+                                  (T[HE][:], T.SelL[:, ev], [HE, "SelL"]), (T[HO][:], T.SelL[:, od], [HO, "SelL"])])
+        cp(T.ll[:], T.pb5[:, 0:128], W=["ll"], B=(5,))
+        cp(T.lh[:], T.pb6[:, 0:128], W=["lh"], B=(6,))
+        msum(T.pb7[:, 0:256], 7, [(T.N0[:], T.R[:], ["N0", "R"]), (T[MW][:], T.SelH[:], [MW, "SelH"]), (T[MW][:], T.SelL[:], [MW, "SelL"])])
+        if t:
+            lengths("rollb")
+            ts(T.sI[:], T.SrI[:], 10, 4095, A.arith_shift_right, A.bitwise_and, R=["SrI"], W=["sI"])
+            ts(T.KT[:, 48:64], T.sI[:], 5.0, None, A.mult, R=["sI"], W=["KT3"])
+            ts(T.npb[:], T.pb2[:, 0:16], 1.0, 16.0, A.add, A.min, W=["npb"], B=(2,))
+        mm(T.pb6[:, 128:256], T.eye[:], T.CH[:], True, False, ["eye", "CH"], (6,))
+        for j in range(8):
+            mm(T.pb6[:, 128 + 16 * j:144 + 16 * j], T["eye" if j < 4 else "e77"][:], T.npb[:], False, j == 7, ["eye", "e77", "npb"], (6,))
+        ts(T.QW[:], T.Q1[:], hl[:, 2048:2049], None, A.mult, R=["Q1"] + kh, W=["QW"])
+        ts(T.TAG[:], T.pb6[:, 128:192], 0.0, BIG, A.is_lt, A.mult, W=["TAG"], B=(6,))
+        tt(T.TAG[:], T.TAG[:], T.TAGC[:], A.add, R=["TAG", "TAGC"], W=["TAG"])
+        for c in range(4):
+            act(T.G[:, 512 * c:512 * c + 512], x.indirect(T.ll[:, 32 * c:32 * c + 32]), R=kx + ["ll"], W=["G%d" % c])
+            if c == 0:
+                act(T.whl[:, 0:256], T.pb7[:, 0:256], W=["wH"], B=(7,))
+                tt(T.whl[:, 256:512], T.pb7[:, 0:256], T.whl[:, 0:256], A.subtract, R=["wH"], W=["wL"], B=(7,))
+            for p, (i, j) in enumerate(PAIRS):
+                o = T["pb%d" % (p // 2)][:, 256 * (p % 2) + 64 * c:256 * (p % 2) + 64 * c + 64]
+                msum(o, p // 2, [(T.eye[:], T.G[:, 512 * c + i:512 * c + 512:8], ["eye", "G%d" % c]),
+                                 (T.neg[:], T.G[:, 512 * c + j:512 * c + 512:8], ["neg", "G%d" % c])])
+        w, W2 = T.win, T.whl
+        mv = []
+        for blk, h in ((0, 1), (1, 3), (2, 8), (4, 0)):
+            o = slice(512 * blk, 512 * blk + 512)
+            if end:
+                mv.append((w[0:128 - h, o], W2[h:128, :]))
+            else:
+                d = 17 - h
+                mv += [(w[d:128, o], W2[0:128 - d, :]), (w[0:d, o], W2[128 - d:128, :])]
+        if not end:
+            table(t + 1)
+        dma("Y", "wi%d" % t, mv, R=["wH", "wL"], W=["win"])
+
+        def gs(c):
+            s = slice(512 * c, 512 * c + 512)
+            tt(T.d8[:, s], x.indirect(T.lh[:, 32 * c:32 * c + 32]), T.G[:, s], A.subtract, R=kx + ["lh", "G%d" % c], W=["d8_%d" % c])
+        gs(0)
+        gs(1)
+        gs(2)
+        run("V", lambda: g.vector.tensor_tensor_scan(T.P[:], T.RM[:], T.G[:], 0.0, A.mult, A.max), ["RM", "G0", "G1", "G2", "G3"], ["P"])
+        for s, e in enumerate((0, 2, 7, 0)):
+            ts(T.Zc[:, 256 * s:256 * s + 256], T.P[:, e:2048:8], -128.0, None, A.add, R=["P"], W=["Zc%d" % s])
+        gs(3)
+
+        def ab(c):
+            act(T.ab8[:, 4 * c:4 * c + 4, :], T.d8[:, 512 * c:512 * c + 512], AF.Abs, R=["d8_%d" % c], W=["ab8_%d" % c])
+
+        def d8sum(hf):
+            msum(T.pb2[:, 64 * hf:64 * hf + 64], 2, [(T.Q1[:, 15 - a:143 - a], T.ab8[:, 8 * hf:8 * hf + 8, 8 * a:8 * a + 8],
+                                                      ["Q1", "ab8_%d" % (2 * hf), "ab8_%d" % (2 * hf + 1)]) for a in range(16)])
+        ab(0)
+        ab(1)
+        d8sum(0)
+        for p in range(4):
+            act(T.ab13[:, 256 * p:256 * p + 256], T["pb%d" % (p // 2)][:, 256 * (p % 2):256 * (p % 2) + 256], AF.Abs, W=["ab13_%d" % p], B=(p // 2,))
+        ab(2)
+        ab(3)
+        zpart = (T.pb4[:, 0:64], 4, [(T.QW[:, 15 - a:143 - a], T.Zc[:, a:1024:16], ["QW", "Zc0", "Zc1", "Zc2", "Zc3"]) for a in range(16)])
+        msum(T.pb3[:, 0:64], 3, [(T.Q1[:, 15 - a:143 - a], T.ab13[:, a:1024:16], ["Q1"] + ["ab13_%d" % p for p in range(4)]) for a in range(16)])
+        msum(zpart[0], zpart[1], zpart[2])
+        d8sum(1)
+
+        def outcomes():
+            tt(T.s4[:], T.pb4[:, 0:64], T.KT[:], A.add, R=["KT", "KT3"], W=["s4"], B=(4,))
+            ts(T.s4[:], T.s4[:], 4095, None, A.bitwise_and, R=["s4"], W=["s4"])
+            tt(T.sq[:], T.s4[:], T.s4[:], A.mult, R=["s4"], W=["sq"])
+            ts(T.f[:], T.s4[:], 1024.0, None, A.mult, R=["s4"], W=["f"])
+            ts(T.sq[:], T.sq[:], 5, None, A.logical_shift_right, R=["sq"], W=["sq"])
+            tt(T.u[:], T.s4[:], T.pb6[:, 192:256], A.add, R=["s4"], W=["u"], B=(6,))
+            tt(T.cand[:], T.TAG[:], T.f[:], A.add, R=["TAG", "f"], W=["cand"])
+            tt(T.u[:], T.u[:], T.sq[:], A.add, R=["u", "sq"], W=["u"])
+            ts(T.u[:], T.u[:], 1023, None, A.bitwise_and, R=["u"], W=["u"])
+            tt(T.cand[:], T.cand[:], T.u[:], A.add, R=["cand", "u"], W=["cand"])
+        if t:
+            tt(T.Bc[:], hl[:, 2049:2050], T.ami[:, 2 * t:2 * t + 1], A.add, R=kh + ["am%d" % t], W=["Bc"])
+        else:
+            cp(T.Bc[:], hl[:, 2049:2050], R=kh, W=["Bc"])
+        ts(T.c13[:], T.pb3[:, 0:64], T.Bc[:], BIG, A.is_gt, A.mult, R=["Bc"], W=["c13"], B=(3,))
+        tt(T.c13[:, 16:32], T.c13[:, 16:32], T.c13[:, 32:48], A.max, R=["c13"], W=["c13"])
+        tt(T.c13[:, 16:32], T.c13[:, 16:32], T.c13[:, 48:64], A.max, R=["c13"], W=["c13"])
+        outcomes()
+        tt(T.e13[:], T.c13[:, 0:32], T.cand[:, 0:32], A.add, R=["c13", "cand"], W=["e13"])
+        tt(T.E[:], T.e13[:, 0:16], T.e13[:, 16:32], A.min, R=["e13"], W=["E"])
+        tt(T.E[:], T.E[:], T.cand[:, 48:64], A.min, R=["E", "cand"], W=["E"])
+        run("V", lambda: g.vector.tensor_tensor_scan(T.M8[:], T.RM[:, 0:128], T.pb2[:, 0:128], 0.0, A.mult, A.max), ["RM"], ["M8"], (2,))
+        ts(T.c8[:], T.M8[:, 7:128:8], T.Bc[:], BIG, A.is_gt, A.mult, R=["M8", "Bc"], W=["c8"])
+        tt(T.c8[:], T.c8[:], T.cand[:, 32:48], A.add, R=["c8", "cand"], W=["c8"])
+        tt(T.SI[:], T.c8[:], T.E[:], A.min, R=["c8", "E"], W=["SI"])
+        tt(T.SF[:], T.c8[:], T.E[:], A.min, R=["c8", "E"], W=["SF"])
+        squares()
+        ts(T.k1[:], T.SI[:], 14, 768, A.arith_shift_right, A.bitwise_and, R=["SI"], W=["k1"])
+        tt(T.k1[:], T.k1[:], T.iB[:], A.add, R=["k1", "iB"], W=["k1"])
+        cp(T.zl[:], T.k1[:], R=["k1"], W=["zl"])
+        act(T.zz[:], T.Zc[:].indirect(T.zl[:]), R=["Zc0", "Zc1", "Zc2", "Zc3", "zl"], W=["zz"], scale=0.5, bias=31.75)
+        if not end:
+            mm(T.pb4[:, 0:16], T.roll[:], T.SF[:], True, True, ["roll", "SF"], (4,))
+            mm(T.pb3[:, 0:16], T.one[:], T.f1[:], True, True, ["one", "f1"], (3,))
+        ts(T.k2[:], T.SI[:], 10, 7 + 16384, A.arith_shift_right, A.bitwise_and, R=["SI"], W=["k2"])
+        tt(T.k2[:], T.k2[:], T.i8[:], A.add, R=["k2", "i8"], W=["k2"])
+        tt(T.k2[:], T.k2[:], T.iB[:], A.max, R=["k2", "iB"], W=["k2"])
+        cp(T.col[:], T.k2[:], R=["k2"], W=["col"])
+
+        if not end:
+            cp(T.SrI[:], T.pb4[:, 0:16], W=["SrI"], B=(4,))
+            ts(T.k3[:], T.SrI[:], 16383, None, A.bitwise_and, R=["SrI"], W=["k3"])
+            cp(T.cl[:], T.k3[:], R=["k3"], W=["cl"])
+            places(T.SrI, "SrI")
+            n = t + 1
+            xn = T["xb%d" % n]
+            ts(T.oldh[:], xn[:].indirect(T.col[:]), 0.5, 32.0, A.mult, A.add, R=["xb%d" % n, "xt%d" % n, "col"], W=["oldh"])
+            tt(xn[:].indirect(T.col[:]), T.oldh[:], T.zz[:], A.add, R=["oldh", "zz", "col"], W=["xb%d" % n])
+            run("V", lambda: g.vector.tensor_reduce(cF[:, 13:14], T.pb3[:, 0:16], AxisListType.X, A.add), (), ["asum"], (3,))
+            ts(T.aI[:], cF[:, 13:14], -0.125, None, A.mult, R=["asum"], W=["aI"])
+            ts(T.amo[:, 2 * n:2 * n + 1], T.aI[:], 15, None, A.bitwise_and, R=["aI", "amo"], W=["amo%d" % n])
+            if t == 0:
+                send("h2", ["hl1"])
+            send("a%d" % n, ["amo", "amo%d" % n])
+            send("x%d" % (n + 1) if n + 1 < TV else "xf", ["xb%d" % n])
+            if n + 2 < TV:
+                send("h%d" % (n + 2), ["hl%d" % (n + 1)])
+
+    send("zf", ["zz"])
+    send("cf", ["col"])
+    places(T.SI, "SI")
+    lengths("eye")
+    cp(T.nls[:], T.pb2[:, 0:16], W=["nls"], B=(2,))
+    act(T.SelH[:], T.win[:].indirect(T.wl[:]), R=["win", "win3", "wl"], W=["SelH"])
+    act(T.SelL[:], T.win[:, 256:2560].indirect(T.wl[:]), R=["win", "win3", "wl"], W=["SelL"])
+    ts(T.IND[:], T.mi[:, 0:32], col(0), None, A.is_gt, R=["mi", "c0"], W=["IND"])
+    cp(T.nst[:, 0:16], T.pb2[:, 0:16], W=["nst"], B=(2,))
+    ts(T.k1[:], T.SI[:], 10, 4095, A.arith_shift_right, A.bitwise_and, R=["SI"], W=["k1"])
+    cp(T.nst[:, 16:32], T.k1[:], R=["k1"], W=["nst2"])
+    run("V", lambda: g.vector.transpose(T.nsx[:], T.nst[:]), ["nst", "nst2"], ["nsx"])
+    tt(T.hs[:], T.SelH[:], T.SelL[:], A.add, R=["SelH", "SelL"], W=["hs"])
+    tt(T.yws[:], T.IND[:].indirect(T.nls[:]), T.hs[:], A.mult, R=["IND", "nls", "hs"], W=["yws"])
+    send("yf", ["yws"])
+    send("nf", ["nsx"])
+    ts(T.oldh[:], T.xf[:].indirect(T.cf[:]), 0.5, 32.0, A.mult, A.add, R=["xf", "xft", "cf"], W=["oldh"])
+    tt(T.xf[:].indirect(T.cf[:]), T.oldh[:], T.zf[:], A.add, R=["oldh", "zf", "cf"], W=["xf"])
+    ts(T.xo[:, 0:1280], T.xf[:, 256:1536], -128.0, None, A.add, R=["xf"], W=["xo0"])
+    act(T.xo[:, 1280:2048], T.xf[:, 1536:NX], R=["xf"], W=["xo1"], bias=-128.0)
+    ys = []
+    for a in range(4):
+        for b in range(2):
+            for k, y in enumerate((T.yn, T.ys)):
+                ys.append((y[2 * a + b:2 * a + b + 1, :], T.nsr[32 * a + 16 * k:32 * a + 16 * k + 16, 16 * b:16 * b + 16]))
+    dma("Y", "o_x0", [(T.yx[:, 0:1280], T.xo[:, 0:1280])], R=["xo0"])
+    dma("S", "o_x1", [(T.yx[:, 1280:2048], T.xo[:, 1280:2048])], R=["xo1"])
+    dma("Y", "o_w", [(T.yw[:], T.ywr[:])], R=["ywr"])
+    dma("Y", "o_ns", ys[0::2], R=["nsr"])
+    dma("S", "o_nt", ys[1::2], R=["nsr"])
+    for s in total:
+        need("Y", (s, total[s]))
+    g.wait_ge(T.sem.L, sent[0])

@@ -2,6 +2,7 @@ from concourse.bass import DstId, RemoteDMATransfer
 from concourse.mybir import AluOpType as A, AxisListType, ActivationFunctionType as AF
 
 TV = 6
+BIG = 5.0 * 2.0 ** 22
 NX = 2304
 NH = 2064
 MATS = ("LOs", "LOq", "HIe", "HIo", "LOe", "LOo", "M1", "LOe0", "LOo0", "HIe0", "HIo0", "M10", "eye", "neg", "N0", "N1", "one")
@@ -30,16 +31,16 @@ for _n, _w, _d in (
         ("kf", 16, "float32"), ("sI", 16, "int32"), ("nF", 16, "float32"), ("f1", 16, "bfloat16"), ("f2", 16, "bfloat16"), ("f3", 16, "bfloat16"),
         ("npb", 16, "bfloat16"), ("Bc", 1, "float32"), ("aI", 1, "int32"), ("amo", 16, "int32"), ("ami", 16, "int32"),
         ("CH", 128, "bfloat16"), ("e77", 128, "bfloat16"),
-        ("nsd", 512, "int32"), ("src8", 768, "bfloat16"), ("e8", 144, "bfloat16"), ("br", 128, "bfloat16"), ("m4", 128, "int32"),
+        ("nsd", 512, "int32"), ("src8", 768, "bfloat16"), ("e8", 144, "bfloat16"), ("br", 128, "bfloat16"), ("ebig", 128, "bfloat16"),
         ("thi", 1, "int32"), ("thb", 1, "bfloat16"), ("wti", 1, "int32"),
-        ("IND", 32, "float32"), ("nls", 16, "uint16"), ("hs", 256, "float32"), ("yws", 256, "float32"), ("ywr", 256, "float32"),
+        ("IND", 32, "float32"), ("m4", 128, "int32"), ("hs", 256, "float32"), ("yws", 256, "float32"), ("ywr", 256, "float32"),
         ("nst", 32, "float32"), ("nsx", 32, "float32"), ("nsr", 32, "float32"), ("xo", 2048, "bfloat16")):
     SCRATCH[_n] = ("sbuf", [128, _w], _d)
 SCRATCH["ab8"] = ("sbuf", [128, 16, 128], "bfloat16")
 
 RING = ["x%d" % t for t in range(1, TV)] + ["h%d" % t for t in range(1, TV)] + ["a%d" % t for t in range(1, TV)]
 FIN = ["xf", "zf", "cf", "yf", "nf"]
-SEMAPHORES = (["V", "S", "P", "G", "L"] + ["r_" + n for n in RING + FIN] + ["tl%d" % t for t in range(TV)] + ["tlb"] + ["wi%d" % t for t in range(TV)]
+SEMAPHORES = (["V", "S", "P", "G", "L", "q"] + ["r_" + n for n in RING + FIN] + ["tl%d" % t for t in range(TV)] + ["tlb", "tlc"] + ["wi%d" % t for t in range(TV)]
               + ["i_" + n for n in ("x", "ls", "wd", "ns", "th", "wt")] + ["o_" + n for n in ("x0", "x1", "w", "ns", "nt")])
 
 
@@ -205,24 +206,19 @@ def rank_program(g, core, T, topo):
 
     dma("S", "i_ls", [(T.lsi[:], T.ls[:])], W=["lsi"])
     dma("Y", "i_ns", [(T.nsd[0:8, 0:256], T.nl[:]), (T.nsd[0:8, 256:512], T.sd[:])], W=["nsd"])
-    dma("Y", "i_wd", [(T.wdi[:], T.wd[:])], W=["wdi"])
-    dma("Y", "i_x", [(T.xr[:], T.x[:])], W=["xr"])
     dma("Y", "i_th", [(T.thi[0:8, :], T.th[:])], W=["thi"])
     dma("Y", "i_wt", [(T.wti[:], T.wt[:])], W=["wti"])
+    dma("Y", "i_x", [(T.xr[:], T.x[:])], W=["xr"])
+    dma("Y", "i_wd", [(T.wdi[:], T.wd[:])], W=["wdi"])
     run("G", lambda: g.iota(T.pc[:], [[0, 1]], 0, 1), (), ["pc"])
     run("G", lambda: g.iota(T.dif[:], [[1, 128]], 256, -1), (), ["dif"])
     run("G", lambda: g.iota(T.mi[:], [[1, 144]], 0, 0), (), ["mi"])
     run("G", lambda: g.iota(T.bi[:], [[16, 16]], 0, 0), (), ["bi"])
-    fill(T.RM[:], 1.0, ["RM"])
-    fill(T.RM[:, 0:2048:8], 0.0, ["RM"])
-    fill(T.TL[:, 0:11264], 0.0, ["TLa"])
-    cp(T.lsH[:], T.lsi[:], R=["lsi"], W=["lsH"])
-    tt(T.lsL[:], T.lsi[:], T.lsH[:], A.subtract, R=["lsi", "lsH"], W=["lsL"])
-    for lo, hi in ((11264, 13312), (13312, 15360), (15360, 16384)):
-        act(T.TL[:, lo:hi], T.RM[:, 0:hi - lo], R=["RM"], W=["TLb"], scale=0.0)
-    zero = ["TLa", "TLb"]
-    dma("Y", "tl0", [(T.TL[a::16, 1024 * a:1024 * a + 1024], T.lsH[a::16, :]) for a in range(16)], R=zero + ["lsH"], W=["TL"])
-    dma("Y", "tlb", [(T.TL[(a + 8) % 16::16, 1024 * a:1024 * a + 1024], T.lsL[a::16, :]) for a in range(16)], R=zero + ["lsL"], W=["TLx"])
+    run("G", lambda: g.iota(T.TL[:, 8192:10240], [[0, 2048]], 0, 0, allow_small_or_imprecise_dtypes=True), (), ["TLc"])
+    fill(T.TL[:, 0:2048], 0.0, ["TLa"])
+    fill(T.TL[:, 2048:8192], 0.0, ["TLd"])
+    for j in range(3):
+        act(T.TL[:, 10240 + 2048 * j:12288 + 2048 * j], T.TL[:, 0:2048], R=["TLa"], W=["TLb%d" % j])
     act(T.xb0[:, 256:NX], T.xr[:], R=["xr"], W=["xb0"], bias=128.0)
 
     cF = T.cF
@@ -233,25 +229,67 @@ def rank_program(g, core, T, topo):
     ts(T.cI[:, 1:2], T.pc[:], 112, None, A.bitwise_and, R=["pc"], W=["cI1"])
     cp(cF[:, 0:2], T.cI[:], R=["cI", "cI1"], W=["c0"])
     ts(T.dif[:], T.dif[:], 127, None, A.bitwise_and, R=["dif"], W=["dif"])
-    ts(col(2), col(1), 15.0, None, A.add, R=["c0"], W=["c2"])
     ts(col(3), col(0), 8.0, None, A.is_lt, R=["c0"], W=["c3"])
     ts(col(4), col(0), 8.0, None, A.is_ge, R=["c0"], W=["c4"])
-    ts(col(6), col(0), 1.0, None, A.is_ge, R=["c0"], W=["c6"])
-    ts(col(7), col(0), 7.0, None, A.is_lt, R=["c0"], W=["c7"])
-    ts(col(9), col(0), 15.0, None, A.is_lt, R=["c0"], W=["c9"])
-    ts(col(11), T.pc[:], 16.0, 15.0, A.mult, A.add, R=["pc"], W=["c11"])
-    cp(col(12), T.pc[:], R=["pc"], W=["c12"])
-    tt(col(5), col(6), col(3), A.mult, R=["c6", "c3"], W=["c5"])
-    tt(col(8), col(9), col(7), A.subtract, R=["c9", "c7"], W=["c8"])
-    ts(T.e8[0:8, :], T.mi[0:8, :], cF[0:8, 11:12], None, A.is_equal, R=["mi", "c11"], W=["e8"])
-    ts(T.m4[0:8, :], T.mi[0:8, 0:128], 4, None, A.logical_shift_right, R=["mi"], W=["m4"])
-    ts(T.br[0:8, :], T.m4[0:8, :], cF[0:8, 12:13], None, A.is_equal, R=["m4", "c12"], W=["br"])
-    ts(T.iB[:], T.bi[:], col(0), None, A.add, R=["bi", "c0"], W=["iB"])
-    ts(T.i8[:], T.iB[:], 8.0, 256.0 - 16384.0, A.mult, A.add, R=["iB"], W=["i8"])
-    ts(T.iBd[:], T.iB[:], 1.0 / 512, None, A.mult, R=["iB"], W=["iBd"])
 
     def mat(name, d, c):
         ts(T[name][:], T.dif[:], float(d), col(c), A.is_equal, A.mult, R=["dif", "c%d" % c], W=[name])
+    mat("LOs", 0, 3)
+    mat("LOq", 8, 3)
+    mat("HIe", 120, 4)
+    mat("HIo", 0, 4)
+    cp(T.lsH[:], T.lsi[:], R=["lsi"], W=["lsH"])
+    tt(T.lsL[:], T.lsi[:], T.lsH[:], A.subtract, R=["lsi", "lsH"], W=["lsL"])
+    zero = ["TLa", "TLb0", "TLb1", "TLb2", "TLc", "TLd"]
+    dma("Y", "tl0", [(T.TL[a::16, 1024 * a:1024 * a + 1024], T.lsH[a::16, :]) for a in range(16)], R=zero + ["lsH"], W=["TL"])
+    for q, sem, key, a0 in (("Y", "tlb", "TLx", 0), ("S", "tlc", "TLy", 8)):
+        dma(q, sem, [(T.TL[(a + 8) % 16::16, 1024 * a:1024 * a + 1024], T.lsL[a::16, :]) for a in range(a0, a0 + 8)],
+            R=zero + ["lsL"], W=[key])
+    cp(col(12), T.pc[:], R=["pc"], W=["c12"])
+    ts(T.m4[0:8, :], T.mi[0:8, 0:128], 4, None, A.logical_shift_right, R=["mi"], W=["m4"])
+    ts(T.br[0:8, :], T.m4[0:8, :], cF[0:8, 12:13], None, A.is_equal, R=["m4", "c12"], W=["br"])
+    cp(T.thb[0:8, :], T.thi[0:8, :], R=["thi"], W=["thb"])
+    mm(T.pb6[:, 0:1], T.br[0:8, :], T.thb[0:8, :], True, True, ["br", "thb"], (6,))
+    def staging(b, l1, l2):
+        for h in range(2):
+            o = 2 * b + h
+            sl = slice(512 * h, 512 * h + 512)
+            msum(T["pb%d" % o][:, 0:512], o, [(T[l1][:], T.lsH[:, sl], [l1, "lsH"]), (T[l2][:], T.lsL[:, sl], [l2, "lsL"])])
+            act(T.hl0[:, 512 * o:512 * o + 512], T["pb%d" % o][:, 0:512], W=["hl0_%d" % o], B=(o,))
+    staging(0, "LOs", "LOq")
+    ts(col(11), T.pc[:], 16.0, 15.0, A.mult, A.add, R=["pc"], W=["c11"])
+    ts(T.e8[0:8, :], T.mi[0:8, :], cF[0:8, 11:12], None, A.is_equal, R=["mi", "c11"], W=["e8"])
+    cp(T.src8[0:8, 0:512], T.nsd[0:8, :], R=["nsd"], W=["src8"])
+    tt(T.src8[0:8, 512:768], T.nsd[0:8, 256:512], T.src8[0:8, 256:512], A.subtract, R=["nsd", "src8"], W=["src8b"])
+    msum(T.pb7[:, 0:48], 7, [(T.e8[0:8, 15 - a:143 - a], T.src8[0:8, a:768:16], ["e8", "src8", "src8b"]) for a in range(16)])
+    staging(1, "HIo", "HIe")
+
+    def sfill(out, c, key):
+        n = out.shape[1]
+        act(out, T.xr[:, 0:n], R=["xr"], W=[key], scale=0.0, bias=float(c))
+
+    def sfills():
+        sfill(T.RM[:], 1.0, "RM")
+        sfill(T.RM[:, 0:2048:8], 0.0, "RM")
+        sfill(T.one[:], 1.0, "one")
+        sfill(T.win[:, 1536:2048], 0.0, "win3")
+    sfill(T.CH[:], 0.0, "CH")
+    for j, (h, v) in enumerate(((1, -2.0 ** 24), (3, -2.0 ** 24 + 2.0 ** 22), (8, -2.0 ** 24 + 2.0 ** 23), (0, 0.0))):
+        sfill(T.TAGC[:, 16 * j:16 * j + 16], v, "TAGC")
+        if h:
+            sfill(T.KT[:, 16 * j:16 * j + 16], h, "KT")
+            sfill(T.CH[:, 16 * j:16 * j + 16], 2.0 * h * BIG + v, "CH")
+            sfill(T.CH[:, 64 + 16 * j:80 + 16 * j], -77.0 * h, "CH")
+    fill(T.hl0[:, 2050:NH], 0.0, ["hl0"])
+    cp(T.hl0[:, 2048:2049], T.wti[:], R=["wti"], W=["hl0w"])
+    cp(T.hl0[:, 2049:2050], T.pb6[:, 0:1], W=["hl0h"], B=(6,))
+    HL0 = ["hl0", "hl0w", "hl0h"] + ["hl0_%d" % o for o in range(4)]
+    ts(col(2), col(1), 15.0, None, A.add, R=["c0"], W=["c2"])
+    ts(col(6), col(0), 1.0, None, A.is_ge, R=["c0"], W=["c6"])
+    ts(col(7), col(0), 7.0, None, A.is_lt, R=["c0"], W=["c7"])
+    ts(col(9), col(0), 15.0, None, A.is_lt, R=["c0"], W=["c9"])
+    tt(col(5), col(6), col(3), A.mult, R=["c6", "c3"], W=["c5"])
+    tt(col(8), col(9), col(7), A.subtract, R=["c9", "c7"], W=["c8"])
 
     def places0():
         ts(T.k2[:], T.sI[:], 15, None, A.bitwise_and, R=["sI"], W=["k2"])
@@ -266,91 +304,58 @@ def rank_program(g, core, T, topo):
         cp(T.cl[:], T.k1[:], R=["k1"], W=["cl"])
         cp(T.SelH[:], T.wdi[:], R=["wdi"], W=["SelH"])
         tt(T.SelL[:], T.wdi[:], T.SelH[:], A.subtract, R=["wdi", "SelH"], W=["SelL"])
-        ts(T.npb[:], T.nF[:], 1.0, 16.0, A.add, A.min, R=["nF"], W=["npb"])
-        fill(T.CH[:], 0.0, ["CH"])
-        for j, h in enumerate((1, 3, 8)):
-            fill(T.CH[:, 16 * j:16 * j + 16], -2.0 * h, ["CH"])
-            fill(T.CH[:, 64 + 16 * j:80 + 16 * j], -77.0 * h, ["CH"])
-        ts(T.e77[:], T.dif[:], 0.0, 77.0, A.is_equal, A.mult, R=["dif"], W=["e77"])
-        ts(T.KT[:, 48:64], T.sI[:], 5.0, None, A.mult, R=["sI"], W=["KT3"])
+        mat("LOe0", 1, 7)
+        mat("LOo0", 9, 7)
+        ts(T.N0[:], T.mi[:, 0:128], col(1), None, A.is_equal, R=["mi", "c0"], W=["N0"])
+        ts(T.N1[:], T.mi[:, 0:128], 8.0, col(1), A.subtract, A.is_equal, R=["mi", "c0"], W=["N1"])
         mat("HIe0", 121, 8)
         mat("HIo0", 1, 8)
-        mat("M10", 1, 9)
+
+    def rest():
         ts(T.eye[:], T.dif[:], 0.0, None, A.is_equal, R=["dif"], W=["eye"])
         ts(T.neg[:], T.dif[:], 0.0, -1.0, A.is_equal, A.mult, R=["dif"], W=["neg"])
+        mat("M10", 1, 9)
+        ts(T.npb[:], T.nF[:], 1.0, 16.0, A.add, A.min, R=["nF"], W=["npb"])
+        ts(T.ebig[:], T.dif[:], 0.0, -BIG, A.is_equal, A.mult, R=["dif"], W=["ebig"])
+        ts(T.e77[:], T.dif[:], 0.0, 77.0, A.is_equal, A.mult, R=["dif"], W=["e77"])
+        ts(T.KT[:, 48:64], T.sI[:], 5.0, None, A.mult, R=["sI"], W=["KT3"])
         ts(T.Q1[:], T.mi[:], col(2), None, A.is_equal, R=["mi", "c2"], W=["Q1"])
-    mat("LOs", 0, 3)
-    mat("LOq", 8, 3)
-    mat("HIe", 120, 4)
-    mat("HIo", 0, 4)
-    cp(T.src8[0:8, 0:512], T.nsd[0:8, :], R=["nsd"], W=["src8"])
-    tt(T.src8[0:8, 512:768], T.nsd[0:8, 256:512], T.src8[0:8, 256:512], A.subtract, R=["nsd", "src8"], W=["src8b"])
-    msum(T.pb7[:, 0:48], 7, [(T.e8[0:8, 15 - a:143 - a], T.src8[0:8, a:768:16], ["e8", "src8", "src8b"]) for a in range(16)])
-    mat("LOe0", 1, 7)
-    mat("LOo0", 9, 7)
-    ts(T.N0[:], T.mi[:, 0:128], col(1), None, A.is_equal, R=["mi", "c0"], W=["N0"])
-    ts(T.N1[:], T.mi[:, 0:128], 8.0, col(1), A.subtract, A.is_equal, R=["mi", "c0"], W=["N1"])
+
+    def last_consts():
+        ts(T.iB[:], T.bi[:], col(0), None, A.add, R=["bi", "c0"], W=["iB"])
+        ts(T.i8[:], T.iB[:], 8.0, 256.0 - 16384.0, A.mult, A.add, R=["iB"], W=["i8"])
+        ts(T.iBd[:], T.iB[:], 1.0 / 512, None, A.mult, R=["iB"], W=["iBd"])
+        ts(T.roll[:], T.dif[:], 16.0, None, A.is_equal, R=["dif"], W=["roll"])
+        ts(T.rollb[:], T.dif[:], 16.0, None, A.is_equal, R=["dif"], W=["rollb"])
+        mat("LOe", 0, 5)
+        mat("LOo", 8, 5)
+        mat("M1", 0, 6)
+        fill(T.amo[:], 0, ["amo"])
     cp(T.nF[:], T.pb7[:, 0:16], W=["nF"], B=(7,))
     cp(T.sI[:], T.pb7[:, 16:32], W=["sI"], B=(7,))
     tt(T.sI[:], T.pb7[:, 32:48], T.sI[:], A.add, R=["sI"], W=["sI"], B=(7,))
     places0()
-    for b, l1, l2 in ((0, "LOs", "LOq"), (1, "HIo", "HIe")):
-        for h in range(2):
-            o = 2 * b + h
-            sl = slice(512 * h, 512 * h + 512)
-            msum(T["pb%d" % o][:, 0:512], o, [(T[l1][:], T.lsH[:, sl], [l1, "lsH"]), (T[l2][:], T.lsL[:, sl], [l2, "lsL"])])
-    for o in range(4):
-        act(T.hl0[:, 512 * o:512 * o + 512], T["pb%d" % o][:, 0:512], W=["hl0_%d" % o], B=(o,))
-    cp(T.thb[0:8, :], T.thi[0:8, :], R=["thi"], W=["thb"])
-    mm(T.pb6[:, 0:1], T.br[0:8, :], T.thb[0:8, :], True, True, ["br", "thb"], (6,))
-    fill(T.hl0[:, 2050:NH], 0.0, ["hl0"])
-    cp(T.hl0[:, 2048:2049], T.wti[:], R=["wti"], W=["hl0w"])
-    cp(T.hl0[:, 2049:2050], T.pb6[:, 0:1], W=["hl0h"], B=(6,))
-    HL0 = ["hl0", "hl0w", "hl0h"] + ["hl0_%d" % o for o in range(4)]
 
     def table(t):
         hl = T["hl%d" % t]
         dma("Y", "tl%d" % t, [(T.TL[p::8, 1024 * (p + 8 * j):1024 * (p + 8 * j) + 1024], hl[p::8, 1024 * j:1024 * j + 1024])
                               for p in range(8) for j in range(2)],
-            R=["hl%d" % t], W=["TL", "TLx"])
+            R=["hl%d" % t], W=["TL", "TLx", "TLy"])
     send("x1", ["xb0", "TL"])
     send("h1", HL0)
     for t in range(1, TV):
         landing("x%d" % t, "xb%d" % t)
         landing("h%d" % t, "hl%d" % t)
         landing("a%d" % t, "am%d" % t)
-        fill(T["xb%d" % t][:, 0:256], 128.0, ["xt%d" % t])
     for n, k in (("xf", "xf"), ("zf", "zf"), ("cf", "cf"), ("yf", "ywr"), ("nf", "nsr")):
         landing(n, k)
-    mat("LOe", 0, 5)
-    mat("LOo", 8, 5)
-    mat("M1", 0, 6)
-    for j, (h, v) in enumerate(((1, -2.0 ** 24), (3, -2.0 ** 24 + 2.0 ** 22), (8, -2.0 ** 24 + 2.0 ** 23), (0, 0.0))):
-        fill(T.TAGC[:, 16 * j:16 * j + 16], v, ["TAGC"])
-        if j < 3:
-            fill(T.KT[:, 16 * j:16 * j + 16], float(h), ["KT"])
-    fill(T.TAG[:], 0.0, ["TAG"])
-    fill(T.win[:, 1536:2048], 0.0, ["win3"])
-    ts(T.roll[:], T.dif[:], 16.0, None, A.is_equal, R=["dif"], W=["roll"])
-    ts(T.rollb[:], T.dif[:], 16.0, None, A.is_equal, R=["dif"], W=["rollb"])
-    fill(T.one[:], 1.0, ["one"])
-    fill(T.amo[:], 0.0, ["amo"])
-    fill(T.xf[:, 0:256], 128.0, ["xft"])
 
-    BIG = 5.0 * 2.0 ** 22
     PAIRS = ((0, 1), (0, 3), (1, 4), (2, 5))
-
-    def places(S, key):
-        ts(T.k1[:], S[:], 22, None, A.arith_shift_right, R=[key], W=["k1"])
-        tt(T.kf[:], T.k1[:], T.iBd[:], A.add, R=["k1", "iBd"], W=["kf"])
-        ts(T.wl[:], T.kf[:], 512.0, 2048.0, A.mult, A.add, R=["kf"], W=["wl"])
 
     def squares():
         ts(T.f1[:], T.SF[:], 0.0, -8.0, A.is_lt, A.mult, R=["SF"], W=["f1"])
 
     def lengths(where):
-        ts(T.f2[:], T.SF[:], -2.0 ** 23, 5.0, A.is_lt, A.mult, R=["SF"], W=["f2"])
-        ts(T.f3[:], T.SF[:], -3.0 * 2.0 ** 22, 2.0, A.is_lt, A.mult, R=["SF"], W=["f3"])
         msum(T.pb2[:, 0:16], 2, [(T[where][:], T[k][:], [where, k]) for k in ("npb", "f1", "f2", "f3")])
 
     for t in range(TV):
@@ -359,7 +364,9 @@ def rank_program(g, core, T, topo):
         x = xb[:, 256:NX]
         hl, kh = T["hl%d" % t], HL0 if t == 0 else ["hl%d" % t]
         LE, LO_, HE, HO, MW = ("LOe0", "LOo0", "HIe0", "HIo0", "M10") if t == 0 else ("LOe", "LOo", "HIe", "HIo", "M1")
-        act(T.R[:], T.TL[:].indirect(T.cl[:]), R=["TL", "TLx", "cl"], W=["R"])
+        act(T.R[:], T.TL[:].indirect(T.cl[:]), R=["TL", "TLx", "TLy", "cl"], W=["R"])
+        if t == 0:
+            sfills()
         if t:
             act(T.SelH[:], T.win[:].indirect(T.wl[:]), R=["win", "win3", "wl"], W=["SelH"])
             act(T.SelL[:], T.win[:, 256:2560].indirect(T.wl[:]), R=["win", "win3", "wl"], W=["SelL"])
@@ -371,21 +378,28 @@ def rank_program(g, core, T, topo):
                                   (T[HE][:], T.SelL[:, ev], [HE, "SelL"]), (T[HO][:], T.SelL[:, od], [HO, "SelL"])])
         cp(T.ll[:], T.pb5[:, 0:128], W=["ll"], B=(5,))
         cp(T.lh[:], T.pb6[:, 0:128], W=["lh"], B=(6,))
+        if t == 0:
+            rest()
         msum(T.pb7[:, 0:256], 7, [(T.N0[:], T.R[:], ["N0", "R"]), (T[MW][:], T.SelH[:], [MW, "SelH"]), (T[MW][:], T.SelL[:], [MW, "SelL"])])
         if t:
             lengths("rollb")
-            ts(T.sI[:], T.SrI[:], 10, 4095, A.arith_shift_right, A.bitwise_and, R=["SrI"], W=["sI"])
             ts(T.KT[:, 48:64], T.sI[:], 5.0, None, A.mult, R=["sI"], W=["KT3"])
-            ts(T.npb[:], T.pb2[:, 0:16], 1.0, 16.0, A.add, A.min, W=["npb"], B=(2,))
-        mm(T.pb6[:, 128:256], T.eye[:], T.CH[:], True, False, ["eye", "CH"], (6,))
-        for j in range(8):
-            mm(T.pb6[:, 128 + 16 * j:144 + 16 * j], T["eye" if j < 4 else "e77"][:], T.npb[:], False, j == 7, ["eye", "e77", "npb"], (6,))
-        ts(T.QW[:], T.Q1[:], hl[:, 2048:2049], None, A.mult, R=["Q1"] + kh, W=["QW"])
-        ts(T.TAG[:], T.pb6[:, 128:192], 0.0, BIG, A.is_lt, A.mult, W=["TAG"], B=(6,))
-        tt(T.TAG[:], T.TAG[:], T.TAGC[:], A.add, R=["TAG", "TAGC"], W=["TAG"])
+        def gs(c):
+            s = slice(512 * c, 512 * c + 512)
+            tt(T.d8[:, s], x.indirect(T.lh[:, 32 * c:32 * c + 32]), T.G[:, s], A.subtract, R=kx + ["lh", "G%d" % c], W=["d8_%d" % c])
         for c in range(4):
-            act(T.G[:, 512 * c:512 * c + 512], x.indirect(T.ll[:, 32 * c:32 * c + 32]), R=kx + ["ll"], W=["G%d" % c])
             if c == 0:
+                act(T.G[:, 0:256], x.indirect(T.ll[:, 0:16]), R=kx + ["ll"], W=["Ga"])
+                act(T.G[:, 256:512], x.indirect(T.ll[:, 16:32]), R=kx + ["ll"], W=["G0"])
+            else:
+                act(T.G[:, 512 * c:512 * c + 512], x.indirect(T.ll[:, 32 * c:32 * c + 32]), R=kx + ["ll"], W=["G%d" % c])
+            if c == 0:
+                ts(T.QW[:], T.Q1[:], hl[:, 2048:2049], None, A.mult, R=["Q1"] + kh, W=["QW"])
+                tt(T.d8[:, 0:256], x.indirect(T.lh[:, 0:16]), T.G[:, 0:256], A.subtract, R=kx + ["lh", "Ga"], W=["d8_a"])
+                tt(T.d8[:, 256:512], x.indirect(T.lh[:, 16:32]), T.G[:, 256:512], A.subtract, R=kx + ["lh", "G0"], W=["d8_0"])
+            elif c < 3:
+                gs(c)
+            if c == 1:
                 act(T.whl[:, 0:256], T.pb7[:, 0:256], W=["wH"], B=(7,))
                 tt(T.whl[:, 256:512], T.pb7[:, 0:256], T.whl[:, 0:256], A.subtract, R=["wH"], W=["wL"], B=(7,))
             for p, (i, j) in enumerate(PAIRS):
@@ -401,26 +415,36 @@ def rank_program(g, core, T, topo):
             else:
                 d = 17 - h
                 mv += [(w[d:128, o], W2[0:128 - d, :]), (w[0:d, o], W2[128 - d:128, :])]
+        dma("Y", "wi%d" % t, mv, R=["wH", "wL"], W=["win"])
         if not end:
             table(t + 1)
-        dma("Y", "wi%d" % t, mv, R=["wH", "wL"], W=["win"])
+        if t == 0:
+            g.sync.sem_inc(T.sem.q, 1)
+            total["q"] = 1
+            need("G", ("q", 1))
+            send("h2", ["hl1"])
+        if t and t + 2 < TV:
+            send("h%d" % (t + 2), ["hl%d" % (t + 1), "win"])
 
-        def gs(c):
-            s = slice(512 * c, 512 * c + 512)
-            tt(T.d8[:, s], x.indirect(T.lh[:, 32 * c:32 * c + 32]), T.G[:, s], A.subtract, R=kx + ["lh", "G%d" % c], W=["d8_%d" % c])
-        gs(0)
-        gs(1)
-        gs(2)
+        if t:
+            ts(T.npb[:], T.pb2[:, 0:16], 1.0, 16.0, A.add, A.min, W=["npb"], B=(2,))
+        mm(T.pb6[:, 128:256], T.eye[:], T.CH[:], True, False, ["eye", "CH"], (6,))
+        for j in range(8):
+            mm(T.pb6[:, 128 + 16 * j:144 + 16 * j], T["ebig" if j < 4 else "e77"][:], T.npb[:], False, j == 7, ["ebig", "e77", "npb"], (6,))
         run("V", lambda: g.vector.tensor_tensor_scan(T.P[:], T.RM[:], T.G[:], 0.0, A.mult, A.max), ["RM", "G0", "G1", "G2", "G3"], ["P"])
+        tt(T.TAG[:], T.pb6[:, 128:192], T.TAGC[:], A.max, R=["TAGC"], W=["TAG"], B=(6,))
         for s, e in enumerate((0, 2, 7, 0)):
             ts(T.Zc[:, 256 * s:256 * s + 256], T.P[:, e:2048:8], -128.0, None, A.add, R=["P"], W=["Zc%d" % s])
         gs(3)
+        if t == 0:
+            last_consts()
 
         def ab(c):
             act(T.ab8[:, 4 * c:4 * c + 4, :], T.d8[:, 512 * c:512 * c + 512], AF.Abs, R=["d8_%d" % c], W=["ab8_%d" % c])
 
         def d8sum(hf):
-            msum(T.pb2[:, 64 * hf:64 * hf + 64], 2, [(T.Q1[:, 15 - a:143 - a], T.ab8[:, 8 * hf:8 * hf + 8, 8 * a:8 * a + 8],
+            bk = (2, 5)[hf]
+            msum(T["pb%d" % bk][:, 0:64], bk, [(T.Q1[:, 15 - a:143 - a], T.ab8[:, 8 * hf:8 * hf + 8, 8 * a:8 * a + 8],
                                                       ["Q1", "ab8_%d" % (2 * hf), "ab8_%d" % (2 * hf + 1)]) for a in range(16)])
         ab(0)
         ab(1)
@@ -429,84 +453,93 @@ def rank_program(g, core, T, topo):
             act(T.ab13[:, 256 * p:256 * p + 256], T["pb%d" % (p // 2)][:, 256 * (p % 2):256 * (p % 2) + 256], AF.Abs, W=["ab13_%d" % p], B=(p // 2,))
         ab(2)
         ab(3)
+        tb = T.xf if end else T["xb%d" % (t + 1)]
+        sfill(tb[:, 0:256], 128.0, "xft" if end else "xt%d" % (t + 1))
         zpart = (T.pb4[:, 0:64], 4, [(T.QW[:, 15 - a:143 - a], T.Zc[:, a:1024:16], ["QW", "Zc0", "Zc1", "Zc2", "Zc3"]) for a in range(16)])
-        msum(T.pb3[:, 0:64], 3, [(T.Q1[:, 15 - a:143 - a], T.ab13[:, a:1024:16], ["Q1"] + ["ab13_%d" % p for p in range(4)]) for a in range(16)])
         msum(zpart[0], zpart[1], zpart[2])
+        msum(T.pb3[:, 0:64], 3, [(T.Q1[:, 15 - a:143 - a], T.ab13[:, a:1024:16], ["Q1"] + ["ab13_%d" % p for p in range(4)]) for a in range(16)])
         d8sum(1)
 
-        def outcomes():
-            tt(T.s4[:], T.pb4[:, 0:64], T.KT[:], A.add, R=["KT", "KT3"], W=["s4"], B=(4,))
-            ts(T.s4[:], T.s4[:], 4095, None, A.bitwise_and, R=["s4"], W=["s4"])
-            tt(T.sq[:], T.s4[:], T.s4[:], A.mult, R=["s4"], W=["sq"])
-            ts(T.f[:], T.s4[:], 1024.0, None, A.mult, R=["s4"], W=["f"])
-            ts(T.sq[:], T.sq[:], 5, None, A.logical_shift_right, R=["sq"], W=["sq"])
-            tt(T.u[:], T.s4[:], T.pb6[:, 192:256], A.add, R=["s4"], W=["u"], B=(6,))
-            tt(T.cand[:], T.TAG[:], T.f[:], A.add, R=["TAG", "f"], W=["cand"])
-            tt(T.u[:], T.u[:], T.sq[:], A.add, R=["u", "sq"], W=["u"])
-            ts(T.u[:], T.u[:], 1023, None, A.bitwise_and, R=["u"], W=["u"])
-            tt(T.cand[:], T.cand[:], T.u[:], A.add, R=["cand", "u"], W=["cand"])
         if t:
             tt(T.Bc[:], hl[:, 2049:2050], T.ami[:, 2 * t:2 * t + 1], A.add, R=kh + ["am%d" % t], W=["Bc"])
         else:
             cp(T.Bc[:], hl[:, 2049:2050], R=kh, W=["Bc"])
+        tt(T.s4[:], T.pb4[:, 0:64], T.KT[:], A.add, R=["KT", "KT3"], W=["s4"], B=(4,))
+        ts(T.s4[:], T.s4[:], 4095, None, A.bitwise_and, R=["s4"], W=["s4"])
+        tt(T.sq[:], T.s4[:], T.s4[:], A.mult, R=["s4"], W=["sq"])
+        ts(T.f[:], T.s4[:], 1024.0, None, A.mult, R=["s4"], W=["f"])
+        ts(T.sq[:], T.sq[:], 5, None, A.logical_shift_right, R=["sq"], W=["sq"])
+        tt(T.u[:], T.s4[:], T.pb6[:, 192:256], A.add, R=["s4"], W=["u"], B=(6,))
+        tt(T.cand[:], T.TAG[:], T.f[:], A.add, R=["TAG", "f"], W=["cand"])
+        tt(T.u[:], T.u[:], T.sq[:], A.add, R=["u", "sq"], W=["u"])
+        run("V", lambda: g.vector.tensor_tensor_scan(T.M8[:, 0:64], T.RM[:, 0:64], T.pb2[:, 0:64], 0.0, A.mult, A.max), ["RM"], ["M8"], (2,))
+        ts(T.u[:], T.u[:], 1023, None, A.bitwise_and, R=["u"], W=["u"])
         ts(T.c13[:], T.pb3[:, 0:64], T.Bc[:], BIG, A.is_gt, A.mult, R=["Bc"], W=["c13"], B=(3,))
+        tt(T.cand[:], T.cand[:], T.u[:], A.add, R=["cand", "u"], W=["cand"])
         tt(T.c13[:, 16:32], T.c13[:, 16:32], T.c13[:, 32:48], A.max, R=["c13"], W=["c13"])
         tt(T.c13[:, 16:32], T.c13[:, 16:32], T.c13[:, 48:64], A.max, R=["c13"], W=["c13"])
-        outcomes()
+        run("V", lambda: g.vector.tensor_tensor_scan(T.M8[:, 64:128], T.RM[:, 0:64], T.pb5[:, 0:64], 0.0, A.mult, A.max), ["RM"], ["M8b"], (5,))
         tt(T.e13[:], T.c13[:, 0:32], T.cand[:, 0:32], A.add, R=["c13", "cand"], W=["e13"])
+        ts(T.c8[:], T.M8[:, 7:128:8], T.Bc[:], BIG, A.is_gt, A.mult, R=["M8", "M8b", "Bc"], W=["c8"])
         tt(T.E[:], T.e13[:, 0:16], T.e13[:, 16:32], A.min, R=["e13"], W=["E"])
-        tt(T.E[:], T.E[:], T.cand[:, 48:64], A.min, R=["E", "cand"], W=["E"])
-        run("V", lambda: g.vector.tensor_tensor_scan(T.M8[:], T.RM[:, 0:128], T.pb2[:, 0:128], 0.0, A.mult, A.max), ["RM"], ["M8"], (2,))
-        ts(T.c8[:], T.M8[:, 7:128:8], T.Bc[:], BIG, A.is_gt, A.mult, R=["M8", "Bc"], W=["c8"])
         tt(T.c8[:], T.c8[:], T.cand[:, 32:48], A.add, R=["c8", "cand"], W=["c8"])
+        tt(T.E[:], T.E[:], T.cand[:, 48:64], A.min, R=["E", "cand"], W=["E"])
         tt(T.SI[:], T.c8[:], T.E[:], A.min, R=["c8", "E"], W=["SI"])
         tt(T.SF[:], T.c8[:], T.E[:], A.min, R=["c8", "E"], W=["SF"])
-        squares()
         ts(T.k1[:], T.SI[:], 14, 768, A.arith_shift_right, A.bitwise_and, R=["SI"], W=["k1"])
+        ts(T.k2[:], T.SI[:], 10, 7 + 16384, A.arith_shift_right, A.bitwise_and, R=["SI"], W=["k2"])
         tt(T.k1[:], T.k1[:], T.iB[:], A.add, R=["k1", "iB"], W=["k1"])
+        tt(T.k2[:], T.k2[:], T.i8[:], A.add, R=["k2", "i8"], W=["k2"])
         cp(T.zl[:], T.k1[:], R=["k1"], W=["zl"])
         act(T.zz[:], T.Zc[:].indirect(T.zl[:]), R=["Zc0", "Zc1", "Zc2", "Zc3", "zl"], W=["zz"], scale=0.5, bias=31.75)
         if not end:
             mm(T.pb4[:, 0:16], T.roll[:], T.SF[:], True, True, ["roll", "SF"], (4,))
-            mm(T.pb3[:, 0:16], T.one[:], T.f1[:], True, True, ["one", "f1"], (3,))
-        ts(T.k2[:], T.SI[:], 10, 7 + 16384, A.arith_shift_right, A.bitwise_and, R=["SI"], W=["k2"])
-        tt(T.k2[:], T.k2[:], T.i8[:], A.add, R=["k2", "i8"], W=["k2"])
-        tt(T.k2[:], T.k2[:], T.iB[:], A.max, R=["k2", "iB"], W=["k2"])
-        cp(T.col[:], T.k2[:], R=["k2"], W=["col"])
-
-        if not end:
+        if end:
+            squares()
+            tt(T.k2[:], T.k2[:], T.iB[:], A.max, R=["k2", "iB"], W=["k2"])
+            cp(T.col[:], T.k2[:], R=["k2"], W=["col"])
+        else:
             cp(T.SrI[:], T.pb4[:, 0:16], W=["SrI"], B=(4,))
             ts(T.k3[:], T.SrI[:], 16383, None, A.bitwise_and, R=["SrI"], W=["k3"])
+            ts(T.sq[:, 0:16], T.SrI[:], 22, None, A.arith_shift_right, R=["SrI"], W=["sq"])
             cp(T.cl[:], T.k3[:], R=["k3"], W=["cl"])
-            places(T.SrI, "SrI")
+            tt(T.kf[:], T.sq[:, 0:16], T.iBd[:], A.add, R=["sq", "iBd"], W=["kf"])
+            tt(T.k2[:], T.k2[:], T.iB[:], A.max, R=["k2", "iB"], W=["k2"])
+            ts(T.wl[:], T.kf[:], 512.0, 2048.0, A.mult, A.add, R=["kf"], W=["wl"])
+            cp(T.col[:], T.k2[:], R=["k2"], W=["col"])
+            squares()
+            mm(T.pb3[:, 0:16], T.one[:], T.f1[:], True, True, ["one", "f1"], (3,))
             n = t + 1
             xn = T["xb%d" % n]
             ts(T.oldh[:], xn[:].indirect(T.col[:]), 0.5, 32.0, A.mult, A.add, R=["xb%d" % n, "xt%d" % n, "col"], W=["oldh"])
             tt(xn[:].indirect(T.col[:]), T.oldh[:], T.zz[:], A.add, R=["oldh", "zz", "col"], W=["xb%d" % n])
             run("V", lambda: g.vector.tensor_reduce(cF[:, 13:14], T.pb3[:, 0:16], AxisListType.X, A.add), (), ["asum"], (3,))
+            ts(T.f2[:], T.SF[:], -2.0 ** 23, 5.0, A.is_lt, A.mult, R=["SF"], W=["f2"])
+            ts(T.f3[:], T.SF[:], -3.0 * 2.0 ** 22, 2.0, A.is_lt, A.mult, R=["SF"], W=["f3"])
             ts(T.aI[:], cF[:, 13:14], -0.125, None, A.mult, R=["asum"], W=["aI"])
+            ts(T.sI[:], T.SrI[:], 10, 4095, A.arith_shift_right, A.bitwise_and, R=["SrI"], W=["sI"])
             ts(T.amo[:, 2 * n:2 * n + 1], T.aI[:], 15, None, A.bitwise_and, R=["aI", "amo"], W=["amo%d" % n])
-            if t == 0:
-                send("h2", ["hl1"])
             send("a%d" % n, ["amo", "amo%d" % n])
             send("x%d" % (n + 1) if n + 1 < TV else "xf", ["xb%d" % n])
-            if n + 2 < TV:
-                send("h%d" % (n + 2), ["hl%d" % (n + 1)])
 
     send("zf", ["zz"])
     send("cf", ["col"])
-    places(T.SI, "SI")
+    ts(T.f2[:], T.SF[:], -2.0 ** 23, 5.0, A.is_lt, A.mult, R=["SF"], W=["f2"])
+    ts(T.f3[:], T.SF[:], -3.0 * 2.0 ** 22, 2.0, A.is_lt, A.mult, R=["SF"], W=["f3"])
+    ts(T.sq[:, 0:16], T.SI[:], 22, None, A.arith_shift_right, R=["SI"], W=["sq"])
     lengths("eye")
-    cp(T.nls[:], T.pb2[:, 0:16], W=["nls"], B=(2,))
+    tt(T.kf[:], T.sq[:, 0:16], T.iBd[:], A.add, R=["sq", "iBd"], W=["kf"])
+    ts(T.k1[:], T.SI[:], 10, 4095, A.arith_shift_right, A.bitwise_and, R=["SI"], W=["k1"])
+    ts(T.wl[:], T.kf[:], 512.0, 2048.0, A.mult, A.add, R=["kf"], W=["wl"])
+    cp(T.cl[:], T.pb2[:, 0:16], W=["cl"], B=(2,))
     act(T.SelH[:], T.win[:].indirect(T.wl[:]), R=["win", "win3", "wl"], W=["SelH"])
     act(T.SelL[:], T.win[:, 256:2560].indirect(T.wl[:]), R=["win", "win3", "wl"], W=["SelL"])
     ts(T.IND[:], T.mi[:, 0:32], col(0), None, A.is_gt, R=["mi", "c0"], W=["IND"])
     cp(T.nst[:, 0:16], T.pb2[:, 0:16], W=["nst"], B=(2,))
-    ts(T.k1[:], T.SI[:], 10, 4095, A.arith_shift_right, A.bitwise_and, R=["SI"], W=["k1"])
     cp(T.nst[:, 16:32], T.k1[:], R=["k1"], W=["nst2"])
     run("V", lambda: g.vector.transpose(T.nsx[:], T.nst[:]), ["nst", "nst2"], ["nsx"])
     tt(T.hs[:], T.SelH[:], T.SelL[:], A.add, R=["SelH", "SelL"], W=["hs"])
-    tt(T.yws[:], T.IND[:].indirect(T.nls[:]), T.hs[:], A.mult, R=["IND", "nls", "hs"], W=["yws"])
+    tt(T.yws[:], T.IND[:].indirect(T.cl[:]), T.hs[:], A.mult, R=["IND", "cl", "hs"], W=["yws"])
     send("yf", ["yws"])
     send("nf", ["nsx"])
     ts(T.oldh[:], T.xf[:].indirect(T.cf[:]), 0.5, 32.0, A.mult, A.add, R=["xf", "xft", "cf"], W=["oldh"])

from concourse.bass import DstId, RemoteDMATransfer
from concourse.mybir import AluOpType as A, AxisListType, ActivationFunctionType as AF

TV = 6
BIG = 5.0 * 2.0 ** 22
NX = 2304
NH = 2064
MATS = ("LOs", "LOq", "HIe", "HIo", "LOe", "LOo", "M1", "LOe0", "LOo0", "HIe0", "HIo0", "M10", "eye", "neg", "N0", "N1", "one")
SCRATCH = {}
for _t in range(TV):
    SCRATCH["xb%d" % _t] = ("sbuf", [128, NX], "bfloat16")
    SCRATCH["hl%d" % _t] = ("sbuf", [128, NH], "bfloat16")
for _m in MATS:
    SCRATCH[_m] = ("sbuf", [128, 128], "bfloat16")
for _b in range(8):
    SCRATCH["pb%d" % _b] = ("psum", [128, 512], "float32")
for _n, _w, _d in (
        ("xf", NX, "bfloat16"), ("xr", 2048, "bfloat16"), ("lsi", 1024, "int32"), ("lsH", 1024, "bfloat16"), ("lsL", 1024, "bfloat16"),
        ("TL", 16384, "bfloat16"), ("win", 2560, "bfloat16"), ("whl", 512, "bfloat16"), ("wdi", 256, "int32"),
        ("G", 2048, "bfloat16"), ("d8", 2048, "bfloat16"), ("P", 2048, "bfloat16"), ("RM", 2048, "bfloat16"), ("Zc", 1024, "bfloat16"),
        ("ab13", 1024, "bfloat16"), ("SelH", 256, "bfloat16"), ("SelL", 256, "bfloat16"), ("R", 256, "bfloat16"),
        ("ll", 128, "uint16"), ("lh", 128, "uint16"), ("zl", 16, "uint16"), ("col", 16, "uint16"), ("wl", 16, "uint16"), ("cl", 16, "uint16"),
        ("zz", 256, "bfloat16"), ("oldh", 256, "bfloat16"), ("zf", 256, "bfloat16"), ("cf", 16, "uint16"),
        ("roll", 128, "float32"), ("Q1", 144, "bfloat16"), ("QW", 144, "bfloat16"), ("rollb", 128, "bfloat16"),
        ("dif", 128, "int32"), ("mi", 144, "int32"), ("pc", 1, "int32"), ("cI", 2, "int32"), ("cF", 16, "float32"),
        ("bi", 16, "int32"), ("iB", 16, "int32"), ("i8", 16, "int32"), ("iBd", 16, "float32"),
        ("KT", 64, "float32"), ("TAGC", 64, "float32"), ("TAG", 64, "float32"),
        ("s4", 64, "int32"), ("sq", 64, "int32"), ("u", 64, "int32"), ("f", 64, "int32"), ("cand", 64, "float32"),
        ("c13", 64, "float32"), ("e13", 32, "float32"), ("E", 16, "float32"), ("M8", 128, "float32"), ("c8", 16, "float32"),
        ("SF", 16, "float32"), ("SI", 16, "int32"), ("SrI", 16, "int32"), ("k1", 16, "int32"), ("k2", 16, "int32"), ("k3", 16, "int32"),
        ("kf", 16, "float32"), ("sI", 16, "int32"), ("nF", 16, "float32"), ("f1", 16, "bfloat16"), ("f2", 16, "bfloat16"), ("f3", 16, "bfloat16"),
        ("npb", 16, "bfloat16"), ("Bc", 1, "float32"), ("aI", 1, "int32"), ("amo", 16, "int32"), ("ami", 16, "int32"),
        ("CH", 128, "bfloat16"), ("e77", 128, "bfloat16"),
        ("nsd", 512, "int32"), ("src8", 768, "bfloat16"), ("e8", 144, "bfloat16"), ("br", 128, "bfloat16"), ("ebig", 128, "bfloat16"),
        ("thi", 1, "int32"), ("thb", 1, "bfloat16"), ("wti", 1, "int32"),
        ("IND", 32, "float32"), ("m4", 128, "int32"), ("hs", 256, "float32"), ("yws", 256, "float32"), ("ywr", 256, "float32"),
        ("nst", 32, "float32"), ("nsx", 32, "float32"), ("nsr", 32, "float32"), ("xo", 2048, "bfloat16")):
    SCRATCH[_n] = ("sbuf", [128, _w], _d)
SCRATCH["ab8"] = ("sbuf", [128, 16, 128], "bfloat16")

RING = ["x%d" % t for t in range(1, TV)] + ["h%d" % t for t in range(1, TV)] + ["a%d" % t for t in range(1, TV)]
FIN = ["xf", "zf", "cf", "yf", "nf"]
SEMAPHORES = (["V", "S", "P", "G", "L", "q"] + ["r_" + n for n in RING + FIN] + ["tl%d" % t for t in range(TV)] + ["tlb", "tlc"] + ["wi%d" % t for t in range(TV)]
              + ["i_" + n for n in ("x", "ls", "wd", "ns", "th", "wt")] + ["o_" + n for n in ("x0", "x1", "w", "ns", "nt")])


def message(name):
    if name in FIN:
        return {"xf": (-5, "xb5", "xf", 256, 2048, 4, 0), "zf": (-6, "zz", "zf", 0, 256, 1, 0), "cf": (-6, "col", "cf", 0, 16, 1, 1),
                "yf": (-5, "yws", "ywr", 0, 256, 1, 2), "nf": (-5, "nsx", "nsr", 0, 32, 1, 3)}[name]
    t = int(name[1:])
    return {"x": (1, "xb%d" % (t - 1), "xb%d" % t, 256, 2048, 4, 0), "h": (1, "hl%d" % (t - 1), "hl%d" % t, 0, NH, 4, 0),
            "a": (1, "amo", "ami", 2 * t, 2, 1, 1)}[name[0]]


def order():
    o = ["x1", "h1", "h2"]
    for t in range(1, TV):
        o.append("a%d" % t)
        o.append("x%d" % (t + 1) if t + 1 < TV else "xf")
        if t + 2 < TV:
            o.append("h%d" % (t + 2))
    return o + ["zf", "cf", "yf", "nf"]


def route(name, src, dst, topo):
    _, _, _, c0, w, pieces, first = message(name)
    if topo.may_write(src, dst):
        return [(None, c0, w)]
    hs = [h for h in topo.cores_of(src) if topo.may_write(h, dst)]
    hs = [h for h in hs if topo.die(h) == topo.die(src)] + [h for h in hs if topo.die(h) != topo.die(src)]
    pieces = min(pieces, len(hs))
    pick = hs[first % len(hs):] + hs[:first % len(hs)]
    return [(pick[j], c0 + w // pieces * j, w // pieces) for j in range(pieces)]


def peer(name, rank):
    return (rank - message(name)[0]) % 8


def put(g, T, topo, core, dst, sem, out, in_):
    rid, pid = topo.addr(dst, core)
    g.remote_dma(out, in_, T.sem[sem], T.sem.L, pid, rid, topo.mask(core, dst))
    return len(topo.engines(core, dst))


def helper_program(g, core, T, topo):
    sent = 0
    for name in order():
        for r in range(8):
            src, dst = T.cores[r], T.cores[peer(name, r)]
            way = route(name, src, dst, topo)
            for h, c0, w in way:
                if h == core:
                    buf = T[message(name)[2]]
                    g.wait_ge(T.sem["r_" + name], len(topo.engines(src, core)) // len(way))
                    sent += put(g, T, topo, core, dst, "r_" + name, buf[:, c0:c0 + w], buf[:, c0:c0 + w])
    if sent:
        g.wait_ge(T.sem.L, sent)


def rank_program(g, core, T, topo):
    rank = T.rank_of(core)
    if rank is None:
        return helper_program(g, core, T, topo)
    Q = {"V": g.vector, "S": g.scalar, "P": g.tensor, "G": g, "Y": g.sync}
    cnt, seen, last, read, bank = {q: 0 for q in Q}, {q: {} for q in Q}, {}, {}, {}
    total = {}

    def need(q, tok):
        sem, val = tok[0], tok[1]
        if seen[q].get(sem, 0) < val:
            Q[q].wait_ge(T.sem[sem], val)
            seen[q][sem] = val

    def deps(q, R, W, B, dma):
        for k in R:
            if k in last:
                need(q, last[k])
        for k in W:
            for tok in ([last[k]] if k in last else []) + list(read.get(k, {}).values()):
                need(q, tok)
        for b in B:
            for q2, tok in bank.get(b, {}).items():
                if q2 != q:
                    need(q, tok)

    def note(q, tok, R, W, B):
        for k in W:
            last[k] = tok
            read[k] = {}
        for k in R:
            if k not in W:
                read.setdefault(k, {})[(tok[2], tok[0])] = tok
        for b in B:
            bank.setdefault(b, {})[q] = tok

    def run(q, call, R=(), W=(), B=()):
        deps(q, R, W, B, False)
        cnt[q] += 1
        call().then_inc(T.sem[q], 1)
        total[q] = cnt[q]
        note(q, (q, cnt[q], q), R, W, B)

    def dma(q, sem, pairs, R=(), W=()):
        deps(q, R, W, (), True)
        for out, in_ in pairs:
            Q[q].dma_start(out, in_).then_inc(T.sem[sem], 16)
            total[sem] = total.get(sem, 0) + 16
        note(q, (sem, total[sem], None), R, W, ())

    sent = [0]

    def send(name, R):
        dst = T.cores[peer(name, rank)]
        sb, db = message(name)[1:3]
        deps("G", R, (), (), True)
        way = route(name, core, dst, topo)
        if len(way) == 1:
            h, c0, w = way[0]
            sent[0] += put(g, T, topo, core, dst if h is None else h, "r_" + name, T[db][:, c0:c0 + w], T[sb][:, c0:c0 + w])
            return
        trs = []
        for j, (h, c0, w) in enumerate(way):
            es = topo.engines(core, h)
            es = es[j * (len(es) // len(way)):(j + 1) * (len(es) // len(way))]
            rid, pid = topo.addr(h, core)
            trs.append(RemoteDMATransfer(dst_ids=[DstId(rid=rid, pnc=pid)], dma_engine_mask=sum(1 << e for e in es),
                                         remote_sem=T.sem["r_" + name], srcs=[T[sb][:, c0:c0 + w]], dsts=[T[db][:, c0:c0 + w]]))
            sent[0] += len(es)
        g.remote_dma_fused(trs, local_sem=T.sem.L)

    def landing(name, key):
        src = T.cores[(rank + message(name)[0]) % 8]
        n = 0
        for h, _, _ in route(name, src, core, topo):
            n += len(topo.engines(src if h is None else h, core))
        last[key] = ("r_" + name, n, None)
        read[key] = {}
        total["r_" + name] = n

    def ts(out, in0, s1, s2, op0, op1=None, R=(), W=(), B=()):
        if op1 is None:
            run("V", lambda: g.vector.tensor_scalar(out, in0, s1, None, op0), R, W, B)
        else:
            run("V", lambda: g.vector.tensor_scalar(out, in0, s1, s2, op0, op1), R, W, B)

    def tt(out, a, b, op, R=(), W=(), B=()):
        run("V", lambda: g.vector.tensor_tensor(out, a, b, op), R, W, B)

    def cp(out, in_, R=(), W=(), B=()):
        run("V", lambda: g.vector.tensor_copy(out, in_), R, W, B)

    def fill(out, c, W, R=()):
        run("V", lambda: g.vector.memset(out, c), R, W)

    def act(out, in_, func=AF.Copy, R=(), W=(), B=(), **kw):
        run("S", lambda: g.scalar.activation(out, in_, func, **kw), R, W, B)

    def mm(out, l, r, start, stop, R=(), B=()):
        run("P", lambda: g.tensor.matmul(out, l, r, start, stop), R, (), B)

    def msum(out, bk, parts):
        for j, (l, r, keys) in enumerate(parts):
            mm(out, l, r, j == 0, j == len(parts) - 1, keys, (bk,))

    dma("S", "i_ls", [(T.lsi[:], T.ls[:])], W=["lsi"])
    dma("Y", "i_ns", [(T.nsd[0:8, 0:256], T.nl[:]), (T.nsd[0:8, 256:512], T.sd[:])], W=["nsd"])
    dma("Y", "i_th", [(T.thi[0:8, :], T.th[:])], W=["thi"])
    dma("Y", "i_wt", [(T.wti[:], T.wt[:])], W=["wti"])
    dma("Y", "i_x", [(T.xr[:], T.x[:])], W=["xr"])
    dma("Y", "i_wd", [(T.wdi[:], T.wd[:])], W=["wdi"])
    run("G", lambda: g.iota(T.pc[:], [[0, 1]], 0, 1), (), ["pc"])
    run("G", lambda: g.iota(T.dif[:], [[1, 128]], 256, -1), (), ["dif"])
    run("G", lambda: g.iota(T.mi[:], [[1, 144]], 0, 0), (), ["mi"])
    run("G", lambda: g.iota(T.bi[:], [[16, 16]], 0, 0), (), ["bi"])
    run("G", lambda: g.iota(T.TL[:, 8192:10240], [[0, 2048]], 0, 0, allow_small_or_imprecise_dtypes=True), (), ["TLc"])
    fill(T.TL[:, 0:2048], 0.0, ["TLa"])
    fill(T.TL[:, 2048:8192], 0.0, ["TLd"])
    for j in range(3):
        act(T.TL[:, 10240 + 2048 * j:12288 + 2048 * j], T.TL[:, 0:2048], R=["TLa"], W=["TLb%d" % j])
    act(T.xb0[:, 256:NX], T.xr[:], R=["xr"], W=["xb0"], bias=128.0)

    cF = T.cF

    def col(j):
        return cF[:, j:j + 1]
    ts(T.cI[:, 0:1], T.pc[:], 15, None, A.bitwise_and, R=["pc"], W=["cI"])
    ts(T.cI[:, 1:2], T.pc[:], 112, None, A.bitwise_and, R=["pc"], W=["cI1"])
    cp(cF[:, 0:2], T.cI[:], R=["cI", "cI1"], W=["c0"])
    ts(T.dif[:], T.dif[:], 127, None, A.bitwise_and, R=["dif"], W=["dif"])
    ts(col(3), col(0), 8.0, None, A.is_lt, R=["c0"], W=["c3"])
    ts(col(4), col(0), 8.0, None, A.is_ge, R=["c0"], W=["c4"])

    def mat(name, d, c):
        ts(T[name][:], T.dif[:], float(d), col(c), A.is_equal, A.mult, R=["dif", "c%d" % c], W=[name])
    mat("LOs", 0, 3)
    mat("LOq", 8, 3)
    mat("HIe", 120, 4)
    mat("HIo", 0, 4)
    cp(T.lsH[:], T.lsi[:], R=["lsi"], W=["lsH"])
    tt(T.lsL[:], T.lsi[:], T.lsH[:], A.subtract, R=["lsi", "lsH"], W=["lsL"])
    zero = ["TLa", "TLb0", "TLb1", "TLb2", "TLc", "TLd"]
    dma("Y", "tl0", [(T.TL[a::16, 1024 * a:1024 * a + 1024], T.lsH[a::16, :]) for a in range(16)], R=zero + ["lsH"], W=["TL"])
    for q, sem, key, a0 in (("Y", "tlb", "TLx", 0), ("S", "tlc", "TLy", 8)):
        dma(q, sem, [(T.TL[(a + 8) % 16::16, 1024 * a:1024 * a + 1024], T.lsL[a::16, :]) for a in range(a0, a0 + 8)],
            R=zero + ["lsL"], W=[key])
    cp(col(12), T.pc[:], R=["pc"], W=["c12"])
    ts(T.m4[0:8, :], T.mi[0:8, 0:128], 4, None, A.logical_shift_right, R=["mi"], W=["m4"])
    ts(T.br[0:8, :], T.m4[0:8, :], cF[0:8, 12:13], None, A.is_equal, R=["m4", "c12"], W=["br"])
    cp(T.thb[0:8, :], T.thi[0:8, :], R=["thi"], W=["thb"])
    mm(T.pb6[:, 0:1], T.br[0:8, :], T.thb[0:8, :], True, True, ["br", "thb"], (6,))
    def staging(b, l1, l2):
        for h in range(2):
            o = 2 * b + h
            sl = slice(512 * h, 512 * h + 512)
            msum(T["pb%d" % o][:, 0:512], o, [(T[l1][:], T.lsH[:, sl], [l1, "lsH"]), (T[l2][:], T.lsL[:, sl], [l2, "lsL"])])
            act(T.hl0[:, 512 * o:512 * o + 512], T["pb%d" % o][:, 0:512], W=["hl0_%d" % o], B=(o,))
    staging(0, "LOs", "LOq")
    ts(col(11), T.pc[:], 16.0, 15.0, A.mult, A.add, R=["pc"], W=["c11"])
    ts(T.e8[0:8, :], T.mi[0:8, :], cF[0:8, 11:12], None, A.is_equal, R=["mi", "c11"], W=["e8"])
    cp(T.src8[0:8, 0:512], T.nsd[0:8, :], R=["nsd"], W=["src8"])
    tt(T.src8[0:8, 512:768], T.nsd[0:8, 256:512], T.src8[0:8, 256:512], A.subtract, R=["nsd", "src8"], W=["src8b"])
    msum(T.pb7[:, 0:48], 7, [(T.e8[0:8, 15 - a:143 - a], T.src8[0:8, a:768:16], ["e8", "src8", "src8b"]) for a in range(16)])
    staging(1, "HIo", "HIe")

    def sfill(out, c, key):
        n = out.shape[1]
        act(out, T.xr[:, 0:n], R=["xr"], W=[key], scale=0.0, bias=float(c))

    def sfills():
        sfill(T.RM[:], 1.0, "RM")
        sfill(T.RM[:, 0:2048:8], 0.0, "RM")
        sfill(T.one[:], 1.0, "one")
        sfill(T.win[:, 1536:2048], 0.0, "win3")
    sfill(T.CH[:], 0.0, "CH")
    for j, (h, v) in enumerate(((1, -2.0 ** 24), (3, -2.0 ** 24 + 2.0 ** 22), (8, -2.0 ** 24 + 2.0 ** 23), (0, 0.0))):
        sfill(T.TAGC[:, 16 * j:16 * j + 16], v, "TAGC")
        if h:
            sfill(T.KT[:, 16 * j:16 * j + 16], h, "KT")
            sfill(T.CH[:, 16 * j:16 * j + 16], 2.0 * h * BIG + v, "CH")
            sfill(T.CH[:, 64 + 16 * j:80 + 16 * j], -77.0 * h, "CH")
    fill(T.hl0[:, 2050:NH], 0.0, ["hl0"])
    cp(T.hl0[:, 2048:2049], T.wti[:], R=["wti"], W=["hl0w"])
    cp(T.hl0[:, 2049:2050], T.pb6[:, 0:1], W=["hl0h"], B=(6,))
    HL0 = ["hl0", "hl0w", "hl0h"] + ["hl0_%d" % o for o in range(4)]
    ts(col(2), col(1), 15.0, None, A.add, R=["c0"], W=["c2"])
    ts(col(6), col(0), 1.0, None, A.is_ge, R=["c0"], W=["c6"])
    ts(col(7), col(0), 7.0, None, A.is_lt, R=["c0"], W=["c7"])
    ts(col(9), col(0), 15.0, None, A.is_lt, R=["c0"], W=["c9"])
    tt(col(5), col(6), col(3), A.mult, R=["c6", "c3"], W=["c5"])
    tt(col(8), col(9), col(7), A.subtract, R=["c9", "c7"], W=["c8"])

    def places0():
        ts(T.k2[:], T.sI[:], 15, None, A.bitwise_and, R=["sI"], W=["k2"])
        tt(T.k1[:], T.sI[:], T.sI[:], A.mult, R=["sI"], W=["k1"])
        ts(T.k1[:], T.k1[:], 5, None, A.logical_shift_right, R=["k1"], W=["k1"])
        tt(T.k1[:], T.k1[:], T.sI[:], A.add, R=["k1", "sI"], W=["k1"])
        ts(T.k3[:], T.nF[:], 77.0, None, A.mult, R=["nF"], W=["k3"])
        tt(T.k1[:], T.k1[:], T.k3[:], A.add, R=["k1", "k3"], W=["k1"])
        ts(T.k1[:], T.k1[:], 1023, None, A.bitwise_and, R=["k1"], W=["k1"])
        ts(T.k2[:], T.k2[:], 1024.0, None, A.mult, R=["k2"], W=["k2"])
        tt(T.k1[:], T.k1[:], T.k2[:], A.add, R=["k1", "k2"], W=["k1"])
        cp(T.cl[:], T.k1[:], R=["k1"], W=["cl"])
        cp(T.SelH[:], T.wdi[:], R=["wdi"], W=["SelH"])
        tt(T.SelL[:], T.wdi[:], T.SelH[:], A.subtract, R=["wdi", "SelH"], W=["SelL"])
        mat("LOe0", 1, 7)
        mat("LOo0", 9, 7)
        ts(T.N0[:], T.mi[:, 0:128], col(1), None, A.is_equal, R=["mi", "c0"], W=["N0"])
        ts(T.N1[:], T.mi[:, 0:128], 8.0, col(1), A.subtract, A.is_equal, R=["mi", "c0"], W=["N1"])
        mat("HIe0", 121, 8)
        mat("HIo0", 1, 8)

    def rest():
        ts(T.eye[:], T.dif[:], 0.0, None, A.is_equal, R=["dif"], W=["eye"])
        ts(T.neg[:], T.dif[:], 0.0, -1.0, A.is_equal, A.mult, R=["dif"], W=["neg"])
        mat("M10", 1, 9)
        ts(T.npb[:], T.nF[:], 1.0, 16.0, A.add, A.min, R=["nF"], W=["npb"])
        ts(T.ebig[:], T.dif[:], 0.0, -BIG, A.is_equal, A.mult, R=["dif"], W=["ebig"])
        ts(T.e77[:], T.dif[:], 0.0, 77.0, A.is_equal, A.mult, R=["dif"], W=["e77"])
        ts(T.KT[:, 48:64], T.sI[:], 5.0, None, A.mult, R=["sI"], W=["KT3"])
        ts(T.Q1[:], T.mi[:], col(2), None, A.is_equal, R=["mi", "c2"], W=["Q1"])

    def last_consts():
        ts(T.iB[:], T.bi[:], col(0), None, A.add, R=["bi", "c0"], W=["iB"])
        ts(T.i8[:], T.iB[:], 8.0, 256.0 - 16384.0, A.mult, A.add, R=["iB"], W=["i8"])
        ts(T.iBd[:], T.iB[:], 1.0 / 512, None, A.mult, R=["iB"], W=["iBd"])
        ts(T.roll[:], T.dif[:], 16.0, None, A.is_equal, R=["dif"], W=["roll"])
        ts(T.rollb[:], T.dif[:], 16.0, None, A.is_equal, R=["dif"], W=["rollb"])
        mat("LOe", 0, 5)
        mat("LOo", 8, 5)
        mat("M1", 0, 6)
        fill(T.amo[:], 0, ["amo"])
    cp(T.nF[:], T.pb7[:, 0:16], W=["nF"], B=(7,))
    cp(T.sI[:], T.pb7[:, 16:32], W=["sI"], B=(7,))
    tt(T.sI[:], T.pb7[:, 32:48], T.sI[:], A.add, R=["sI"], W=["sI"], B=(7,))
    places0()

    def table(t):
        hl = T["hl%d" % t]
        dma("Y", "tl%d" % t, [(T.TL[p::8, 1024 * (p + 8 * j):1024 * (p + 8 * j) + 1024], hl[p::8, 1024 * j:1024 * j + 1024])
                              for p in range(8) for j in range(2)],
            R=["hl%d" % t], W=["TL", "TLx", "TLy"])
    send("x1", ["xb0", "TL"])
    send("h1", HL0)
    for t in range(1, TV):
        landing("x%d" % t, "xb%d" % t)
        landing("h%d" % t, "hl%d" % t)
        landing("a%d" % t, "am%d" % t)
    for n, k in (("xf", "xf"), ("zf", "zf"), ("cf", "cf"), ("yf", "ywr"), ("nf", "nsr")):
        landing(n, k)

    PAIRS = ((0, 1), (0, 3), (1, 4), (2, 5))

    def squares():
        ts(T.f1[:], T.SF[:], 0.0, -8.0, A.is_lt, A.mult, R=["SF"], W=["f1"])

    def lengths(where):
        msum(T.pb2[:, 0:16], 2, [(T[where][:], T[k][:], [where, k]) for k in ("npb", "f1", "f2", "f3")])

    for t in range(TV):
        end = t == TV - 1
        xb, kx = T["xb%d" % t], ["xb%d" % t]
        x = xb[:, 256:NX]
        hl, kh = T["hl%d" % t], HL0 if t == 0 else ["hl%d" % t]
        LE, LO_, HE, HO, MW = ("LOe0", "LOo0", "HIe0", "HIo0", "M10") if t == 0 else ("LOe", "LOo", "HIe", "HIo", "M1")
        act(T.R[:], T.TL[:].indirect(T.cl[:]), R=["TL", "TLx", "TLy", "cl"], W=["R"])
        if t == 0:
            sfills()
        if t:
            act(T.SelH[:], T.win[:].indirect(T.wl[:]), R=["win", "win3", "wl"], W=["SelH"])
            act(T.SelL[:], T.win[:, 256:2560].indirect(T.wl[:]), R=["win", "win3", "wl"], W=["SelL"])
        ev, od = slice(0, 256, 2), slice(1, 256, 2)
        msum(T.pb5[:, 0:128], 5, [(T.N0[:], T.R[:, ev], ["N0", "R"]), (T.N1[:], T.R[:, od], ["N1", "R"]),
                                  (T[LE][:], T.SelH[:, ev], [LE, "SelH"]), (T[LO_][:], T.SelH[:, od], [LO_, "SelH"]),
                                  (T[LE][:], T.SelL[:, ev], [LE, "SelL"]), (T[LO_][:], T.SelL[:, od], [LO_, "SelL"])])
        msum(T.pb6[:, 0:128], 6, [(T[HE][:], T.SelH[:, ev], [HE, "SelH"]), (T[HO][:], T.SelH[:, od], [HO, "SelH"]),
                                  (T[HE][:], T.SelL[:, ev], [HE, "SelL"]), (T[HO][:], T.SelL[:, od], [HO, "SelL"])])
        cp(T.ll[:], T.pb5[:, 0:128], W=["ll"], B=(5,))
        cp(T.lh[:], T.pb6[:, 0:128], W=["lh"], B=(6,))
        if t == 0:
            rest()
        msum(T.pb7[:, 0:256], 7, [(T.N0[:], T.R[:], ["N0", "R"]), (T[MW][:], T.SelH[:], [MW, "SelH"]), (T[MW][:], T.SelL[:], [MW, "SelL"])])
        if t:
            lengths("rollb")
            ts(T.KT[:, 48:64], T.sI[:], 5.0, None, A.mult, R=["sI"], W=["KT3"])
        def gs(c):
            s = slice(512 * c, 512 * c + 512)
            tt(T.d8[:, s], x.indirect(T.lh[:, 32 * c:32 * c + 32]), T.G[:, s], A.subtract, R=kx + ["lh", "G%d" % c], W=["d8_%d" % c])
        for c in range(4):
            if c == 0:
                act(T.G[:, 0:256], x.indirect(T.ll[:, 0:16]), R=kx + ["ll"], W=["Ga"])
                act(T.G[:, 256:512], x.indirect(T.ll[:, 16:32]), R=kx + ["ll"], W=["G0"])
            else:
                act(T.G[:, 512 * c:512 * c + 512], x.indirect(T.ll[:, 32 * c:32 * c + 32]), R=kx + ["ll"], W=["G%d" % c])
            if c == 0:
                ts(T.QW[:], T.Q1[:], hl[:, 2048:2049], None, A.mult, R=["Q1"] + kh, W=["QW"])
                tt(T.d8[:, 0:256], x.indirect(T.lh[:, 0:16]), T.G[:, 0:256], A.subtract, R=kx + ["lh", "Ga"], W=["d8_a"])
                tt(T.d8[:, 256:512], x.indirect(T.lh[:, 16:32]), T.G[:, 256:512], A.subtract, R=kx + ["lh", "G0"], W=["d8_0"])
            elif c < 3:
                gs(c)
            if c == 1:
                act(T.whl[:, 0:256], T.pb7[:, 0:256], W=["wH"], B=(7,))
                tt(T.whl[:, 256:512], T.pb7[:, 0:256], T.whl[:, 0:256], A.subtract, R=["wH"], W=["wL"], B=(7,))
            for p, (i, j) in enumerate(PAIRS):
                o = T["pb%d" % (p // 2)][:, 256 * (p % 2) + 64 * c:256 * (p % 2) + 64 * c + 64]
                msum(o, p // 2, [(T.eye[:], T.G[:, 512 * c + i:512 * c + 512:8], ["eye", "G%d" % c]),
                                 (T.neg[:], T.G[:, 512 * c + j:512 * c + 512:8], ["neg", "G%d" % c])])
        w, W2 = T.win, T.whl
        mv = []
        for blk, h in ((0, 1), (1, 3), (2, 8), (4, 0)):
            o = slice(512 * blk, 512 * blk + 512)
            if end:
                mv.append((w[0:128 - h, o], W2[h:128, :]))
            else:
                d = 17 - h
                mv += [(w[d:128, o], W2[0:128 - d, :]), (w[0:d, o], W2[128 - d:128, :])]
        dma("Y", "wi%d" % t, mv, R=["wH", "wL"], W=["win"])
        if not end:
            table(t + 1)
        if t == 0:
            g.sync.sem_inc(T.sem.q, 1)
            total["q"] = 1
            need("G", ("q", 1))
            send("h2", ["hl1"])
        if t and t + 2 < TV:
            send("h%d" % (t + 2), ["hl%d" % (t + 1), "win"])

        if t:
            ts(T.npb[:], T.pb2[:, 0:16], 1.0, 16.0, A.add, A.min, W=["npb"], B=(2,))
        mm(T.pb6[:, 128:256], T.eye[:], T.CH[:], True, False, ["eye", "CH"], (6,))
        for j in range(8):
            mm(T.pb6[:, 128 + 16 * j:144 + 16 * j], T["ebig" if j < 4 else "e77"][:], T.npb[:], False, j == 7, ["ebig", "e77", "npb"], (6,))
        run("V", lambda: g.vector.tensor_tensor_scan(T.P[:], T.RM[:], T.G[:], 0.0, A.mult, A.max), ["RM", "G0", "G1", "G2", "G3"], ["P"])
        tt(T.TAG[:], T.pb6[:, 128:192], T.TAGC[:], A.max, R=["TAGC"], W=["TAG"], B=(6,))
        for s, e in enumerate((0, 2, 7, 0)):
            ts(T.Zc[:, 256 * s:256 * s + 256], T.P[:, e:2048:8], -128.0, None, A.add, R=["P"], W=["Zc%d" % s])
        gs(3)
        if t == 0:
            last_consts()

        def ab(c):
            act(T.ab8[:, 4 * c:4 * c + 4, :], T.d8[:, 512 * c:512 * c + 512], AF.Abs, R=["d8_%d" % c], W=["ab8_%d" % c])

        def d8sum(hf):
            bk = (2, 5)[hf]
            msum(T["pb%d" % bk][:, 0:64], bk, [(T.Q1[:, 15 - a:143 - a], T.ab8[:, 8 * hf:8 * hf + 8, 8 * a:8 * a + 8],
                                                      ["Q1", "ab8_%d" % (2 * hf), "ab8_%d" % (2 * hf + 1)]) for a in range(16)])
        ab(0)
        ab(1)
        d8sum(0)
        for p in range(4):
            act(T.ab13[:, 256 * p:256 * p + 256], T["pb%d" % (p // 2)][:, 256 * (p % 2):256 * (p % 2) + 256], AF.Abs, W=["ab13_%d" % p], B=(p // 2,))
        ab(2)
        ab(3)
        tb = T.xf if end else T["xb%d" % (t + 1)]
        sfill(tb[:, 0:256], 128.0, "xft" if end else "xt%d" % (t + 1))
        zpart = (T.pb4[:, 0:64], 4, [(T.QW[:, 15 - a:143 - a], T.Zc[:, a:1024:16], ["QW", "Zc0", "Zc1", "Zc2", "Zc3"]) for a in range(16)])
        msum(zpart[0], zpart[1], zpart[2])
        msum(T.pb3[:, 0:64], 3, [(T.Q1[:, 15 - a:143 - a], T.ab13[:, a:1024:16], ["Q1"] + ["ab13_%d" % p for p in range(4)]) for a in range(16)])
        d8sum(1)

        if t:
            tt(T.Bc[:], hl[:, 2049:2050], T.ami[:, 2 * t:2 * t + 1], A.add, R=kh + ["am%d" % t], W=["Bc"])
        else:
            cp(T.Bc[:], hl[:, 2049:2050], R=kh, W=["Bc"])
        tt(T.s4[:], T.pb4[:, 0:64], T.KT[:], A.add, R=["KT", "KT3"], W=["s4"], B=(4,))
        ts(T.s4[:], T.s4[:], 4095, None, A.bitwise_and, R=["s4"], W=["s4"])
        tt(T.sq[:], T.s4[:], T.s4[:], A.mult, R=["s4"], W=["sq"])
        ts(T.f[:], T.s4[:], 1024.0, None, A.mult, R=["s4"], W=["f"])
        ts(T.sq[:], T.sq[:], 5, None, A.logical_shift_right, R=["sq"], W=["sq"])
        tt(T.u[:], T.s4[:], T.pb6[:, 192:256], A.add, R=["s4"], W=["u"], B=(6,))
        tt(T.cand[:], T.TAG[:], T.f[:], A.add, R=["TAG", "f"], W=["cand"])
        tt(T.u[:], T.u[:], T.sq[:], A.add, R=["u", "sq"], W=["u"])
        run("V", lambda: g.vector.tensor_tensor_scan(T.M8[:, 0:64], T.RM[:, 0:64], T.pb2[:, 0:64], 0.0, A.mult, A.max), ["RM"], ["M8"], (2,))
        ts(T.u[:], T.u[:], 1023, None, A.bitwise_and, R=["u"], W=["u"])
        ts(T.c13[:], T.pb3[:, 0:64], T.Bc[:], BIG, A.is_gt, A.mult, R=["Bc"], W=["c13"], B=(3,))
        tt(T.cand[:], T.cand[:], T.u[:], A.add, R=["cand", "u"], W=["cand"])
        tt(T.c13[:, 16:32], T.c13[:, 16:32], T.c13[:, 32:48], A.max, R=["c13"], W=["c13"])
        tt(T.c13[:, 16:32], T.c13[:, 16:32], T.c13[:, 48:64], A.max, R=["c13"], W=["c13"])
        run("V", lambda: g.vector.tensor_tensor_scan(T.M8[:, 64:128], T.RM[:, 0:64], T.pb5[:, 0:64], 0.0, A.mult, A.max), ["RM"], ["M8b"], (5,))
        tt(T.e13[:], T.c13[:, 0:32], T.cand[:, 0:32], A.add, R=["c13", "cand"], W=["e13"])
        ts(T.c8[:], T.M8[:, 7:128:8], T.Bc[:], BIG, A.is_gt, A.mult, R=["M8", "M8b", "Bc"], W=["c8"])
        tt(T.E[:], T.e13[:, 0:16], T.e13[:, 16:32], A.min, R=["e13"], W=["E"])
        tt(T.c8[:], T.c8[:], T.cand[:, 32:48], A.add, R=["c8", "cand"], W=["c8"])
        tt(T.E[:], T.E[:], T.cand[:, 48:64], A.min, R=["E", "cand"], W=["E"])
        tt(T.SI[:], T.c8[:], T.E[:], A.min, R=["c8", "E"], W=["SI"])
        tt(T.SF[:], T.c8[:], T.E[:], A.min, R=["c8", "E"], W=["SF"])
        ts(T.k1[:], T.SI[:], 14, 768, A.arith_shift_right, A.bitwise_and, R=["SI"], W=["k1"])
        ts(T.k2[:], T.SI[:], 10, 7 + 16384, A.arith_shift_right, A.bitwise_and, R=["SI"], W=["k2"])
        tt(T.k1[:], T.k1[:], T.iB[:], A.add, R=["k1", "iB"], W=["k1"])
        tt(T.k2[:], T.k2[:], T.i8[:], A.add, R=["k2", "i8"], W=["k2"])
        cp(T.zl[:], T.k1[:], R=["k1"], W=["zl"])
        act(T.zz[:], T.Zc[:].indirect(T.zl[:]), R=["Zc0", "Zc1", "Zc2", "Zc3", "zl"], W=["zz"], scale=0.5, bias=31.75)
        if not end:
            mm(T.pb4[:, 0:16], T.roll[:], T.SF[:], True, True, ["roll", "SF"], (4,))
        if end:
            squares()
            tt(T.k2[:], T.k2[:], T.iB[:], A.max, R=["k2", "iB"], W=["k2"])
            cp(T.col[:], T.k2[:], R=["k2"], W=["col"])
        else:
            cp(T.SrI[:], T.pb4[:, 0:16], W=["SrI"], B=(4,))
            ts(T.k3[:], T.SrI[:], 16383, None, A.bitwise_and, R=["SrI"], W=["k3"])
            ts(T.sq[:, 0:16], T.SrI[:], 22, None, A.arith_shift_right, R=["SrI"], W=["sq"])
            cp(T.cl[:], T.k3[:], R=["k3"], W=["cl"])
            tt(T.kf[:], T.sq[:, 0:16], T.iBd[:], A.add, R=["sq", "iBd"], W=["kf"])
            tt(T.k2[:], T.k2[:], T.iB[:], A.max, R=["k2", "iB"], W=["k2"])
            ts(T.wl[:], T.kf[:], 512.0, 2048.0, A.mult, A.add, R=["kf"], W=["wl"])
            cp(T.col[:], T.k2[:], R=["k2"], W=["col"])
            squares()
            mm(T.pb3[:, 0:16], T.one[:], T.f1[:], True, True, ["one", "f1"], (3,))
            n = t + 1
            xn = T["xb%d" % n]
            ts(T.oldh[:], xn[:].indirect(T.col[:]), 0.5, 32.0, A.mult, A.add, R=["xb%d" % n, "xt%d" % n, "col"], W=["oldh"])
            tt(xn[:].indirect(T.col[:]), T.oldh[:], T.zz[:], A.add, R=["oldh", "zz", "col"], W=["xb%d" % n])
            run("V", lambda: g.vector.tensor_reduce(cF[:, 13:14], T.pb3[:, 0:16], AxisListType.X, A.add), (), ["asum"], (3,))
            ts(T.f2[:], T.SF[:], -2.0 ** 23, 5.0, A.is_lt, A.mult, R=["SF"], W=["f2"])
            ts(T.f3[:], T.SF[:], -3.0 * 2.0 ** 22, 2.0, A.is_lt, A.mult, R=["SF"], W=["f3"])
            ts(T.aI[:], cF[:, 13:14], -0.125, None, A.mult, R=["asum"], W=["aI"])
            ts(T.sI[:], T.SrI[:], 10, 4095, A.arith_shift_right, A.bitwise_and, R=["SrI"], W=["sI"])
            ts(T.amo[:, 2 * n:2 * n + 1], T.aI[:], 15, None, A.bitwise_and, R=["aI", "amo"], W=["amo%d" % n])
            send("a%d" % n, ["amo", "amo%d" % n])
            send("x%d" % (n + 1) if n + 1 < TV else "xf", ["xb%d" % n])

    send("zf", ["zz"])
    send("cf", ["col"])
    ts(T.f2[:], T.SF[:], -2.0 ** 23, 5.0, A.is_lt, A.mult, R=["SF"], W=["f2"])
    ts(T.f3[:], T.SF[:], -3.0 * 2.0 ** 22, 2.0, A.is_lt, A.mult, R=["SF"], W=["f3"])
    ts(T.sq[:, 0:16], T.SI[:], 22, None, A.arith_shift_right, R=["SI"], W=["sq"])
    lengths("eye")
    tt(T.kf[:], T.sq[:, 0:16], T.iBd[:], A.add, R=["sq", "iBd"], W=["kf"])
    ts(T.k1[:], T.SI[:], 10, 4095, A.arith_shift_right, A.bitwise_and, R=["SI"], W=["k1"])
    ts(T.wl[:], T.kf[:], 512.0, 2048.0, A.mult, A.add, R=["kf"], W=["wl"])
    cp(T.cl[:], T.pb2[:, 0:16], W=["cl"], B=(2,))
    act(T.SelH[:], T.win[:].indirect(T.wl[:]), R=["win", "win3", "wl"], W=["SelH"])
    act(T.SelL[:], T.win[:, 256:2560].indirect(T.wl[:]), R=["win", "win3", "wl"], W=["SelL"])
    ts(T.IND[:], T.mi[:, 0:32], col(0), None, A.is_gt, R=["mi", "c0"], W=["IND"])
    cp(T.nst[:, 0:16], T.pb2[:, 0:16], W=["nst"], B=(2,))
    cp(T.nst[:, 16:32], T.k1[:], R=["k1"], W=["nst2"])
    run("V", lambda: g.vector.transpose(T.nsx[:], T.nst[:]), ["nst", "nst2"], ["nsx"])
    tt(T.hs[:], T.SelH[:], T.SelL[:], A.add, R=["SelH", "SelL"], W=["hs"])
    tt(T.yws[:], T.IND[:].indirect(T.cl[:]), T.hs[:], A.mult, R=["IND", "cl", "hs"], W=["yws"])
    send("yf", ["yws"])
    send("nf", ["nsx"])
    ts(T.oldh[:], T.xf[:].indirect(T.cf[:]), 0.5, 32.0, A.mult, A.add, R=["xf", "xft", "cf"], W=["oldh"])
    tt(T.xf[:].indirect(T.cf[:]), T.oldh[:], T.zf[:], A.add, R=["oldh", "zf", "cf"], W=["xf"])
    ts(T.xo[:, 0:1280], T.xf[:, 256:1536], -128.0, None, A.add, R=["xf"], W=["xo0"])
    act(T.xo[:, 1280:2048], T.xf[:, 1536:NX], R=["xf"], W=["xo1"], bias=-128.0)
    ys = []
    for a in range(4):
        for b in range(2):
            for k, y in enumerate((T.yn, T.ys)):
                ys.append((y[2 * a + b:2 * a + b + 1, :], T.nsr[32 * a + 16 * k:32 * a + 16 * k + 16, 16 * b:16 * b + 16]))
    dma("Y", "o_x0", [(T.yx[:, 0:1280], T.xo[:, 0:1280])], R=["xo0"])
    dma("S", "o_x1", [(T.yx[:, 1280:2048], T.xo[:, 1280:2048])], R=["xo1"])
    dma("Y", "o_w", [(T.yw[:], T.ywr[:])], R=["ywr"])
    dma("Y", "o_ns", ys[0::2], R=["nsr"])
    dma("S", "o_nt", ys[1::2], R=["nsr"])
    for s in total:
        need("Y", (s, total[s]))
    g.wait_ge(T.sem.L, sent[0])
